import numpy as np
import ml_dtypes


def mxq(x, axis, fmt="e4m3"):
    dtype, down = {"e4m3": (ml_dtypes.float8_e4m3fn, 7), "e5m2": (ml_dtypes.float8_e5m2, 14)}[fmt]
    v = np.moveaxis(np.asarray(x, np.float32).astype(ml_dtypes.bfloat16).astype(np.float64), axis, -1)
    blocks = v.reshape(v.shape[:-1] + (-1, 32))
    amax = np.abs(blocks).max(-1, keepdims=True)
    byte = np.maximum(np.where(amax > 0, np.frexp(amax)[1] - 1 + 127, 0) - down, 1)
    scale = np.exp2(byte - 127.0)
    codes = (blocks / scale).astype(np.float32).astype(dtype).astype(np.float64)
    return np.moveaxis((codes * scale).reshape(v.shape), -1, axis)


WIDE = False


def mx_kscale(k):
    if not WIDE:
        return np.ones(k)
    levels = np.array([10, -10, 5, -5, 0])
    if k % 512:
        return np.exp2(np.random.permutation(np.resize(levels, k // 32))).repeat(32)
    a = np.empty((k // 512, 16))
    for p in range(k // 512):
        a[p, :8] = np.random.permutation(np.resize(levels, 8))
        for g in range(8):
            far = levels[np.abs(levels - a[p, g]) >= 10]
            a[p, g + 8] = far[np.random.randint(len(far))]
    return np.exp2(a.ravel()).repeat(32)


def f64(x):
    return np.asarray(x).astype(np.float64)


def striped(idx):
    return np.tile(np.asarray(idx).reshape(-1, 16).T, (8, 1)).astype(np.uint16)


def unstriped(offs):
    return offs[:16].T.reshape(-1).astype(np.int64)


E2M1 = np.array([0.0, 0.5, 1.0, 1.5, 2.0, 3.0, 4.0, 6.0, -0.0, -0.5, -1.0, -1.5, -2.0, -3.0, -4.0, -6.0])


def pack_weight(w, fmt):
    k, n = w.shape
    w = f64(np.asarray(w, np.float32).astype(ml_dtypes.bfloat16)).reshape(k // 32, 32, n)
    amax = np.abs(w).max(1)
    if fmt == "e4m3":
        byte = np.frexp(amax)[1] - 1 + 127 - 7
    else:
        mant, ex = np.frexp(amax / 6.0)
        byte = np.where(mant > 0.5, ex, ex - 1) + 127
    byte = np.clip(np.where(amax > 0, byte, 1), 1, 254)
    scaled = (w * np.exp2(127.0 - byte)[:, None, :]).reshape(k, n).astype(np.float32)
    by_word = np.ascontiguousarray(scaled.reshape(k // 512, 128, 4, n).transpose(0, 1, 3, 2))
    if fmt == "e4m3":
        words = by_word.astype(ml_dtypes.float8_e4m3fn).view(np.uint8)
    else:
        c = by_word.astype(ml_dtypes.float4_e2m1fn).view(np.uint8) & 0xF
        words = (c[..., 0::2] | (c[..., 1::2] << 4)).reshape(k // 512, 128, 2 * n)
    return np.ascontiguousarray(words), np.ascontiguousarray(byte.astype(np.uint8).reshape(k // 512, 16, n))


def unpack_weight(words, scales, fmt):
    g, _, n = scales.shape
    words = np.ascontiguousarray(words).reshape(g, 128, n, -1)
    if fmt == "e4m3":
        vals = words.view(ml_dtypes.float8_e4m3fn).astype(np.float64)
    else:
        nib = np.empty((g, 128, n, 4), np.uint8)
        nib[..., 0::2] = words & 0xF
        nib[..., 1::2] = words >> 4
        vals = E2M1[nib]
    vals = vals * np.repeat(np.exp2(scales.astype(np.float64) - 127.0), 8, axis=1)[..., None]
    return vals.transpose(0, 1, 3, 2).reshape(g * 512, n)


D, T, I, Q, E = 512, 2048, 512, 256, 512


def setup_inputs():
    n = np.random.standard_normal
    idx = np.random.permutation(T)[:I]
    fd = mx_kscale(D)
    fi = mx_kscale(I)
    ti = np.ones(T)
    ti[idx] = fi
    keysp = pack_weight(n((D, T)) / fd[:, None], "e4m3")
    return {
        "query": (n((D, Q)) * 0.5 / np.sqrt(D) * fd[:, None]).astype(np.float32),
        "keys_words": keysp[0],
        "keys_scales": keysp[1],
        "fac": (np.random.uniform(0.5, 2.0, (I, 1)) * fi[:, None]).astype(np.float32),
        "vals": (n((E, T)) / ti).astype(np.float32),
        "offs": striped(idx),
    }


def reference(query, keys_words, keys_scales, fac, vals, offs):
    idx = unstriped(offs)
    keysu = unpack_weight(keys_words, keys_scales, "e4m3")
    keysidxg = keysu[:, idx]
    queryq = mxq(f64(query), 0, "e4m3")
    a = keysidxg.T @ queryq
    p = np.exp(a - np.max(a, axis=1, keepdims=True))
    w = p * f64(fac) / np.sum(p, axis=1, keepdims=True)
    vt = f64(vals)[:, idx].T
    wq = mxq(w, 0, "e4m3")
    vtq = mxq(vt, 0, "e4m3")
    o = wq.T @ vtq
    return o

@@ -1,0 +1,195 @@
+from contextlib import ExitStack
+
+import concourse.mybir as mybir
+from concourse.masks import make_identity
+
+D, T, I, Q, E = 512, 2048, 512, 256, 512
+FLOPS = 2 * D * I * Q + 2 * I * Q * E
+
+F32 = mybir.dt.float32
+BF16 = mybir.dt.bfloat16
+I32 = mybir.dt.int32
+U32 = mybir.dt.uint32
+U16 = mybir.dt.uint16
+U8 = mybir.dt.uint8
+FP8X4 = mybir.dt.float8_e4m3fn_x4
+ALU = mybir.AluOpType
+ACT = mybir.ActivationFunctionType
+AX = mybir.AxisListType
+
+P = 128
+PACK = 4
+BLOCKS = E // P
+HALVES = Q // P
+
+
+def interleave(copy, dst, src):
+    copy(
+        out=dst.rearrange("p (c i) t -> p c t i", i=4),
+        in_=src.rearrange("p t (c i) -> p c t i", i=4),
+    )
+
+
+def tile_attend_slotattn_kernel(tc, query, keys_words, keys_scales, fac, vals, offs, out):
+    nc = tc.nc
+    with ExitStack() as ctx:
+        keep = ctx.enter_context(tc.tile_pool(name="keep", bufs=1))
+        psum = ctx.enter_context(tc.psum_pool(name="psum", bufs=1))
+
+        def sbuf(name, shape, dtype, tag=None):
+            return keep.tile(shape, dtype, name=name, tag=tag or name, align_bytes=64)
+
+        offsets = keep.tile([P, I // 16], U16, name="offsets")
+        nc.sync.dma_start(offsets[:], offs)
+
+        q_raw = sbuf("q_raw", [P, PACK, Q], F32)
+        nc.sync.dma_start(out=q_raw[:], in_=query.rearrange("(p j) q -> p j q", j=PACK))
+
+        ks_pool = sbuf("ks_pool", [P, T], U8)
+        nc.gpsimd.memset(ks_pool[:].bitcast(I32), 0)
+        for quad in range(4):
+            nc.scalar.dma_start(
+                out=ks_pool[32 * quad : 32 * quad + 4, :].bitcast(I32),
+                in_=keys_scales[0, 4 * quad : 4 * quad + 4, :].bitcast(I32),
+            )
+
+        kw_pool = sbuf("kw_pool", [P, T], U32)
+        nc.sync.dma_start(
+            out=kw_pool[:].bitcast(I32),
+            in_=keys_words[0].rearrange("p n t -> p (n t)").bitcast(I32),
+        )
+
+        fac_sb = sbuf("fac_sb", [P, PACK], F32)
+        nc.scalar.dma_start(out=fac_sb[:], in_=fac.rearrange("(p t) o -> p (t o)", t=PACK))
+
+        ident = sbuf("ident", [P, P], F32)
+        make_identity(nc, ident[:])
+
+        v_pool = {}
+
+        def load_values(c, tag):
+            v_pool[c] = sbuf(f"v_pool{c}", [P, T], F32, tag)
+            nc.sync.dma_start(out=v_pool[c][:], in_=vals[c * P : (c + 1) * P, :])
+
+        load_values(0, None)
+
+        q_bf = sbuf("q_bf", [P, Q, PACK], BF16)
+        interleave(nc.scalar.copy, q_bf[:], q_raw[:])
+        load_values(1, "q_raw")
+
+        ks_listed = sbuf("ks_listed", [P, I], U8)
+        nc.vector.tensor_copy(ks_listed[:], ks_pool[:].indirect(offsets[:]))
+        load_values(2, "ks_pool")
+        k_scales = sbuf("k_scales", [P, PACK, P], U8)
+        nc.vector.tensor_copy(k_scales[:], ks_listed[:].rearrange("p (s t) -> p t s", t=PACK))
+        q_codes = sbuf("q_codes", [P, Q], U32, "ks_listed")
+        q_scales = sbuf("q_scales", [P, Q], U8)
+        nc.vector.quantize_mx(
+            out=q_codes[:].bitcast(FP8X4), scales=q_scales[:], in_=q_bf[:].rearrange("p q t -> p (q t)")
+        )
+        k_codes = sbuf("k_codes", [P, PACK, P], U32, "q_bf")
+        nc.vector.tensor_copy(k_codes[:].rearrange("p t s -> p s t"), kw_pool[:].indirect(offsets[:]))
+        load_values(3, "kw_pool")
+
+        neg_max = sbuf("neg_max", [P, PACK], F32)
+        row_sum = sbuf("row_sum", [P, PACK], F32)
+        probs = sbuf("probs", [P, PACK, Q], F32)
+        for t in range(PACK):
+            scores = psum.tile([P, Q], F32, name=f"scores{t}", tag=f"bank{t}")
+            nc.tensor.matmul_mx(
+                out=scores[:],
+                lhsT=k_codes[:, t, :].bitcast(FP8X4),
+                lhsT_scale=k_scales[:, t, :],
+                rhs=q_codes[:].bitcast(FP8X4),
+                rhs_scale=q_scales[:],
+                start=True,
+                stop=True,
+            )
+            nc.vector.tensor_reduce(out=neg_max[:, t : t + 1], in_=scores[:], axis=AX.X, op=ALU.max, negate=True)
+            nc.scalar.activation(
+                out=probs[:, t, :],
+                in_=scores[:],
+                func=ACT.Exp,
+                bias=neg_max[:, t : t + 1],
+                accum_out=row_sum[:, t : t + 1],
+            )
+
+        def gather(c, tag):
+            listed = sbuf(f"v_listed{c}", [P, I], BF16, tag)
+            nc.vector.tensor_copy(listed[:], v_pool[c][:].indirect(offsets[:]))
+            return listed
+
+        def turn(listed, vt_bf):
+            pairs = listed[:].bitcast(F32)
+            turned = psum.tile([P, 2, P], F32, name="turned", tag="turned", bufs=2)
+            for u in range(2):
+                nc.tensor.transpose(turned[:, u, :], pairs[:, u : I // 2 : 2], ident[:])
+            nc.scalar.copy(out=vt_bf.bitcast(F32), in_=turned[:].rearrange("p u e -> p e u"))
+
+        def quantize(name, tag, values):
+            width = values.shape[1]
+            codes = sbuf(name + "_codes", [P, width], U32, tag)
+            scales = sbuf(name + "_scales", [P, width], U8)
+            nc.vector.quantize_mx(
+                out=codes[:].bitcast(FP8X4), scales=scales[:], in_=values.rearrange("p e t -> p (e t)")
+            )
+            return codes, scales
+
+        listed0 = gather(0, "q_bf")
+        inv_sum = sbuf("inv_sum", [P, PACK], F32, "v_pool0")
+        nc.vector.reciprocal(out=inv_sum[:], in_=row_sum[:])
+        row_factor = sbuf("row_factor", [P, PACK], F32)
+        nc.vector.tensor_tensor(out=row_factor[:], in0=inv_sum[:], in1=fac_sb[:], op=ALU.mult)
+        w_rows = sbuf("w_rows", [P, PACK, Q], BF16)
+        for t in range(PACK):
+            nc.scalar.activation(
+                out=w_rows[:, t, :], in_=probs[:, t, :], func=ACT.Copy, scale=row_factor[:, t : t + 1]
+            )
+        listed1 = gather(1, "v_pool0")
+        w_bf = sbuf("w_bf", [P, Q, PACK], BF16)
+        interleave(nc.scalar.copy, w_bf[:], w_rows[:])
+        vt01 = sbuf("vt01", [P, 2 * P, PACK], BF16, "w_rows")
+        turn(listed0, vt01[:, 0:P, :])
+        turn(listed1, vt01[:, P : 2 * P, :])
+        listed2 = gather(2, "q_raw")
+        vt2 = sbuf("vt2", [P, P, PACK], BF16)
+        turn(listed2, vt2[:])
+        w_codes, w_scales = quantize("w", "ks_pool", w_bf[:])
+        v01 = quantize("v01", "w_bf", vt01[:])
+
+        out_rows = out.rearrange("(h p) e -> p h e", p=P)
+
+        def product(acc, h, values):
+            v_codes, v_scales = values
+            nc.tensor.matmul_mx(
+                out=acc,
+                lhsT=w_codes[:, h * P : (h + 1) * P].bitcast(FP8X4),
+                lhsT_scale=w_scales[:, h * P : (h + 1) * P],
+                rhs=v_codes[:].bitcast(FP8X4),
+                rhs_scale=v_scales[:],
+                start=True,
+                stop=True,
+            )
+
+        def both_halves(name, values, first, bank):
+            width = values[0].shape[1]
+            acc = psum.tile([P, HALVES, width], F32, name=name + "_acc", tag=bank)
+            for h in range(HALVES):
+                product(acc[:, h, :], h, values)
+            result = sbuf(name + "_out", [P, HALVES, width], F32)
+            nc.scalar.copy(out=result[:], in_=acc[:])
+            nc.sync.dma_start(out=out_rows[:, :, first : first + width], in_=result[:])
+
+        both_halves("early", v01, 0, "bank0")
+        listed3 = gather(3, "w_rows")
+        vt3 = sbuf("vt3", [P, P, PACK], BF16)
+        turn(listed3, vt3[:])
+        v2 = quantize("v2", "kw_pool", vt2[:])
+        v3 = quantize("v3", None, vt3[:])
+        both_halves("third", v2, 2 * P, "bank1")
+        for h, (copy, queue) in enumerate(((nc.vector.tensor_copy, nc.sync), (nc.scalar.copy, nc.scalar))):
+            acc_h = psum.tile([P, P], F32, name=f"acc_last{h}", tag=f"bank{2 + h}")
+            product(acc_h[:], h, v3)
+            late_out = sbuf(f"late_out{h}", [P, P], F32)
+            copy(out=late_out[:], in_=acc_h[:])
+            queue.dma_start(out=out_rows[:, h, 3 * P : 4 * P], in_=late_out[:])

@@ -48,7 +48,7 @@ def tile_attend_slotattn_kernel(tc, query, keys_words, keys_scales, fac, vals, o
         ks_pool = sbuf("ks_pool", [P, T], U8)
         nc.gpsimd.memset(ks_pool[:].bitcast(I32), 0)
         for quad in range(4):
-            nc.scalar.dma_start(
+            nc.sync.dma_start(
                 out=ks_pool[32 * quad : 32 * quad + 4, :].bitcast(I32),
                 in_=keys_scales[0, 4 * quad : 4 * quad + 4, :].bitcast(I32),
             )
@@ -80,13 +80,13 @@ def tile_attend_slotattn_kernel(tc, query, keys_words, keys_scales, fac, vals, o
         ks_listed = sbuf("ks_listed", [P, I], U8)
         nc.vector.tensor_copy(ks_listed[:], ks_pool[:].indirect(offsets[:]))
         load_values(2, "ks_pool")
-        k_scales = sbuf("k_scales", [P, PACK, P], U8)
-        nc.vector.tensor_copy(k_scales[:], ks_listed[:].rearrange("p (s t) -> p t s", t=PACK))
-        q_codes = sbuf("q_codes", [P, Q], U32, "ks_listed")
+        q_codes = sbuf("q_codes", [P, Q], U32)
         q_scales = sbuf("q_scales", [P, Q], U8)
         nc.vector.quantize_mx(
             out=q_codes[:].bitcast(FP8X4), scales=q_scales[:], in_=q_bf[:].rearrange("p q t -> p (q t)")
         )
+        k_scales = sbuf("k_scales", [P, PACK, P], U8)
+        nc.vector.tensor_copy(k_scales[:], ks_listed[:].rearrange("p (s t) -> p t s", t=PACK))
         k_codes = sbuf("k_codes", [P, PACK, P], U32, "q_bf")
         nc.vector.tensor_copy(k_codes[:].rearrange("p t s -> p s t"), kw_pool[:].indirect(offsets[:]))
         load_values(3, "kw_pool")
@@ -136,26 +136,26 @@ def tile_attend_slotattn_kernel(tc, query, keys_words, keys_scales, fac, vals, o
             return codes, scales
 
         listed0 = gather(0, "q_bf")
+        vt0 = sbuf("vt0", [P, P, PACK], BF16)
+        turn(listed0, vt0[:])
         inv_sum = sbuf("inv_sum", [P, PACK], F32, "v_pool0")
         nc.vector.reciprocal(out=inv_sum[:], in_=row_sum[:])
         row_factor = sbuf("row_factor", [P, PACK], F32)
         nc.vector.tensor_tensor(out=row_factor[:], in0=inv_sum[:], in1=fac_sb[:], op=ALU.mult)
-        w_rows = sbuf("w_rows", [P, PACK, Q], BF16)
+        w_rows = sbuf("w_rows", [P, PACK, Q], BF16, "q_bf")
         for t in range(PACK):
             nc.scalar.activation(
                 out=w_rows[:, t, :], in_=probs[:, t, :], func=ACT.Copy, scale=row_factor[:, t : t + 1]
             )
-        listed1 = gather(1, "v_pool0")
+        listed1 = gather(1, "row_sum")
+        v0 = quantize("v0", "q_raw", vt0[:])
         w_bf = sbuf("w_bf", [P, Q, PACK], BF16)
         interleave(nc.scalar.copy, w_bf[:], w_rows[:])
-        vt01 = sbuf("vt01", [P, 2 * P, PACK], BF16, "w_rows")
-        turn(listed0, vt01[:, 0:P, :])
-        turn(listed1, vt01[:, P : 2 * P, :])
-        listed2 = gather(2, "q_raw")
-        vt2 = sbuf("vt2", [P, P, PACK], BF16)
-        turn(listed2, vt2[:])
+        vt12 = sbuf("vt12", [P, 2 * P, PACK], BF16, "q_bf")
+        turn(listed1, vt12[:, 0:P, :])
+        listed2 = gather(2, None)
+        turn(listed2, vt12[:, P : 2 * P, :])
         w_codes, w_scales = quantize("w", "ks_pool", w_bf[:])
-        v01 = quantize("v01", "w_bf", vt01[:])
 
         out_rows = out.rearrange("(h p) e -> p h e", p=P)
 
@@ -180,13 +180,13 @@ def tile_attend_slotattn_kernel(tc, query, keys_words, keys_scales, fac, vals, o
             nc.scalar.copy(out=result[:], in_=acc[:])
             nc.sync.dma_start(out=out_rows[:, :, first : first + width], in_=result[:])
 
-        both_halves("early", v01, 0, "bank0")
-        listed3 = gather(3, "w_rows")
+        both_halves("first", v0, 0, "bank0")
+        listed3 = gather(3, None)
         vt3 = sbuf("vt3", [P, P, PACK], BF16)
         turn(listed3, vt3[:])
-        v2 = quantize("v2", "kw_pool", vt2[:])
+        v12 = quantize("v12", "kw_pool", vt12[:])
         v3 = quantize("v3", None, vt3[:])
-        both_halves("third", v2, 2 * P, "bank1")
+        both_halves("middle", v12, P, "bank1")
         for h, (copy, queue) in enumerate(((nc.vector.tensor_copy, nc.sync), (nc.scalar.copy, nc.scalar))):
             acc_h = psum.tile([P, P], F32, name=f"acc_last{h}", tag=f"bank{2 + h}")
             product(acc_h[:], h, v3)

@@ -91,8 +91,10 @@ def tile_attend_slotattn_kernel(tc, query, keys_words, keys_scales, fac, vals, o
         nc.vector.tensor_copy(k_codes[:].rearrange("p t s -> p s t"), kw_pool[:].indirect(offsets[:]))
         load_values(3, "kw_pool")
 
-        neg_max = sbuf("neg_max", [P, PACK], F32)
-        row_sum = sbuf("row_sum", [P, PACK], F32)
+        listed0 = sbuf("v_listed0", [P, I], BF16)
+        words0 = listed0[:].bitcast(F32)
+        neg_max = [words0[:, (t // 2) * P + t % 2 : (t // 2) * P + t % 2 + 1] for t in range(PACK)]
+        row_sum = [sbuf(f"row_sum{u}", [P, 2], F32) for u in range(2)]
         probs = sbuf("probs", [P, PACK, Q], F32)
         for t in range(PACK):
             scores = psum.tile([P, Q], F32, name=f"scores{t}", tag=f"bank{t}")
@@ -105,13 +107,13 @@ def tile_attend_slotattn_kernel(tc, query, keys_words, keys_scales, fac, vals, o
                 start=True,
                 stop=True,
             )
-            nc.vector.tensor_reduce(out=neg_max[:, t : t + 1], in_=scores[:], axis=AX.X, op=ALU.max, negate=True)
+            nc.vector.tensor_reduce(out=neg_max[t], in_=scores[:], axis=AX.X, op=ALU.max, negate=True)
             nc.scalar.activation(
                 out=probs[:, t, :],
                 in_=scores[:],
                 func=ACT.Exp,
-                bias=neg_max[:, t : t + 1],
-                accum_out=row_sum[:, t : t + 1],
+                bias=neg_max[t],
+                accum_out=row_sum[t // 2][:, t % 2 : t % 2 + 1],
             )
 
         def gather(c, tag):
@@ -133,29 +135,38 @@ def tile_attend_slotattn_kernel(tc, query, keys_words, keys_scales, fac, vals, o
             nc.vector.quantize_mx(
                 out=codes[:].bitcast(FP8X4), scales=scales[:], in_=values.rearrange("p e t -> p (e t)")
             )
-            return codes, scales
+            return codes[:], scales[:]
 
-        listed0 = gather(0, "q_bf")
-        vt0 = sbuf("vt0", [P, P, PACK], BF16)
-        turn(listed0, vt0[:])
-        inv_sum = sbuf("inv_sum", [P, PACK], F32, "v_pool0")
-        nc.vector.reciprocal(out=inv_sum[:], in_=row_sum[:])
-        row_factor = sbuf("row_factor", [P, PACK], F32)
-        nc.vector.tensor_tensor(out=row_factor[:], in0=inv_sum[:], in1=fac_sb[:], op=ALU.mult)
-        w_rows = sbuf("w_rows", [P, PACK, Q], BF16, "q_bf")
-        for t in range(PACK):
-            nc.scalar.activation(
-                out=w_rows[:, t, :], in_=probs[:, t, :], func=ACT.Copy, scale=row_factor[:, t : t + 1]
+        w_rows = sbuf("w_rows", [P, PACK, Q], BF16)
+        for u in range(2):
+            inv_sum = sbuf(f"inv_sum{u}", [P, 2], F32)
+            nc.vector.reciprocal(out=inv_sum[:], in_=row_sum[u][:])
+            nc.vector.tensor_copy(
+                listed0[:, u * (I // 2) : (u + 1) * (I // 2)],
+                v_pool[0][:].indirect(offsets[:, u * (I // 32) : (u + 1) * (I // 32)]),
             )
-        listed1 = gather(1, "row_sum")
-        v0 = quantize("v0", "q_raw", vt0[:])
-        w_bf = sbuf("w_bf", [P, Q, PACK], BF16)
-        interleave(nc.scalar.copy, w_bf[:], w_rows[:])
-        vt12 = sbuf("vt12", [P, 2 * P, PACK], BF16, "q_bf")
-        turn(listed1, vt12[:, 0:P, :])
-        listed2 = gather(2, None)
-        turn(listed2, vt12[:, P : 2 * P, :])
-        w_codes, w_scales = quantize("w", "ks_pool", w_bf[:])
+            row_factor = sbuf(f"row_factor{u}", [P, 2], F32)
+            nc.vector.tensor_tensor(
+                out=row_factor[:], in0=inv_sum[:], in1=fac_sb[:, 2 * u : 2 * u + 2], op=ALU.mult
+            )
+            for b in range(2):
+                nc.scalar.activation(
+                    out=w_rows[:, 2 * u + b, :],
+                    in_=probs[:, 2 * u + b, :],
+                    func=ACT.Copy,
+                    scale=row_factor[:, b : b + 1],
+                )
+        wv_bf = sbuf("wv_bf", [P, Q + 2 * P, PACK], BF16)
+        turn(listed0, wv_bf[:, Q : Q + P, :])
+        interleave(nc.scalar.copy, wv_bf[:, 0:Q, :], w_rows[:])
+        listed1 = gather(1, "row_sum1")
+        turn(listed1, wv_bf[:, Q + P : Q + 2 * P, :])
+        listed2 = gather(2, "inv_sum1")
+        vt2 = sbuf("vt2", [P, P, PACK], BF16)
+        turn(listed2, vt2[:])
+        wv_codes, wv_scales = quantize("wv", "ks_pool", wv_bf[:])
+        w_codes, w_scales = wv_codes[:, 0:Q], wv_scales[:, 0:Q]
+        v01 = wv_codes[:, Q : Q + 2 * P], wv_scales[:, Q : Q + 2 * P]
 
         out_rows = out.rearrange("(h p) e -> p h e", p=P)
 
@@ -165,8 +176,8 @@ def tile_attend_slotattn_kernel(tc, query, keys_words, keys_scales, fac, vals, o
                 out=acc,
                 lhsT=w_codes[:, h * P : (h + 1) * P].bitcast(FP8X4),
                 lhsT_scale=w_scales[:, h * P : (h + 1) * P],
-                rhs=v_codes[:].bitcast(FP8X4),
-                rhs_scale=v_scales[:],
+                rhs=v_codes.bitcast(FP8X4),
+                rhs_scale=v_scales,
                 start=True,
                 stop=True,
             )
@@ -180,13 +191,13 @@ def tile_attend_slotattn_kernel(tc, query, keys_words, keys_scales, fac, vals, o
             nc.scalar.copy(out=result[:], in_=acc[:])
             nc.sync.dma_start(out=out_rows[:, :, first : first + width], in_=result[:])
 
-        both_halves("first", v0, 0, "bank0")
+        both_halves("first", v01, 0, "bank0")
         listed3 = gather(3, None)
         vt3 = sbuf("vt3", [P, P, PACK], BF16)
         turn(listed3, vt3[:])
-        v12 = quantize("v12", "kw_pool", vt12[:])
+        v2 = quantize("v2", "kw_pool", vt2[:])
+        both_halves("middle", v2, 2 * P, "bank1")
         v3 = quantize("v3", None, vt3[:])
-        both_halves("middle", v12, P, "bank1")
         for h, (copy, queue) in enumerate(((nc.vector.tensor_copy, nc.sync), (nc.scalar.copy, nc.scalar))):
             acc_h = psum.tile([P, P], F32, name=f"acc_last{h}", tag=f"bank{2 + h}")
             product(acc_h[:], h, v3)

@@ -47,10 +47,10 @@ def tile_attend_slotattn_kernel(tc, query, keys_words, keys_scales, fac, vals, o
 
         ks_pool = sbuf("ks_pool", [P, T], U8)
         nc.gpsimd.memset(ks_pool[:].bitcast(I32), 0)
-        for quad in range(4):
+        for r in range(4):
             nc.sync.dma_start(
-                out=ks_pool[32 * quad : 32 * quad + 4, :].bitcast(I32),
-                in_=keys_scales[0, 4 * quad : 4 * quad + 4, :].bitcast(I32),
+                out=ks_pool[r:P:32, :].bitcast(I32),
+                in_=keys_scales[0, r:16:4, :].bitcast(I32),
             )
 
         kw_pool = sbuf("kw_pool", [P, T], U32)
@@ -138,16 +138,21 @@ def tile_attend_slotattn_kernel(tc, query, keys_words, keys_scales, fac, vals, o
             return codes[:], scales[:]
 
         w_rows = sbuf("w_rows", [P, PACK, Q], BF16)
-        for u in range(2):
-            inv_sum = sbuf(f"inv_sum{u}", [P, 2], F32)
-            nc.vector.reciprocal(out=inv_sum[:], in_=row_sum[u][:])
+        inv_sum = [sbuf(f"inv_sum{u}", [P, 2], F32) for u in range(2)]
+
+        def gather_half(u):
             nc.vector.tensor_copy(
                 listed0[:, u * (I // 2) : (u + 1) * (I // 2)],
                 v_pool[0][:].indirect(offsets[:, u * (I // 32) : (u + 1) * (I // 32)]),
             )
+
+        nc.vector.reciprocal(out=inv_sum[0][:], in_=row_sum[0][:])
+        gather_half(0)
+        nc.vector.reciprocal(out=inv_sum[1][:], in_=row_sum[1][:])
+        for u in range(2):
             row_factor = sbuf(f"row_factor{u}", [P, 2], F32)
             nc.vector.tensor_tensor(
-                out=row_factor[:], in0=inv_sum[:], in1=fac_sb[:, 2 * u : 2 * u + 2], op=ALU.mult
+                out=row_factor[:], in0=inv_sum[u][:], in1=fac_sb[:, 2 * u : 2 * u + 2], op=ALU.mult
             )
             for b in range(2):
                 nc.scalar.activation(
@@ -156,6 +161,7 @@ def tile_attend_slotattn_kernel(tc, query, keys_words, keys_scales, fac, vals, o
                     func=ACT.Copy,
                     scale=row_factor[:, b : b + 1],
                 )
+        gather_half(1)
         wv_bf = sbuf("wv_bf", [P, Q + 2 * P, PACK], BF16)
         turn(listed0, wv_bf[:, Q : Q + P, :])
         interleave(nc.scalar.copy, wv_bf[:, 0:Q, :], w_rows[:])

@@ -41,9 +41,11 @@ def tile_attend_slotattn_kernel(tc, query, keys_words, keys_scales, fac, vals, o
 
         offsets = keep.tile([P, I // 16], U16, name="offsets")
         nc.sync.dma_start(offsets[:], offs)
+        fac_sb = sbuf("fac_sb", [P, PACK], F32)
+        nc.sync.dma_start(out=fac_sb[:], in_=fac.rearrange("(p t) o -> p (t o)", t=PACK))
 
         q_raw = sbuf("q_raw", [P, PACK, Q], F32)
-        nc.sync.dma_start(out=q_raw[:], in_=query.rearrange("(p j) q -> p j q", j=PACK))
+        nc.scalar.dma_start(out=q_raw[:], in_=query.rearrange("(p j) q -> p j q", j=PACK))
 
         ks_pool = sbuf("ks_pool", [P, T], U8)
         nc.gpsimd.memset(ks_pool[:].bitcast(I32), 0)
@@ -58,9 +60,6 @@ def tile_attend_slotattn_kernel(tc, query, keys_words, keys_scales, fac, vals, o
             out=kw_pool[:].bitcast(I32),
             in_=keys_words[0].rearrange("p n t -> p (n t)").bitcast(I32),
         )
-
-        fac_sb = sbuf("fac_sb", [P, PACK], F32)
-        nc.scalar.dma_start(out=fac_sb[:], in_=fac.rearrange("(p t) o -> p (t o)", t=PACK))
 
         ident = sbuf("ident", [P, P], F32)
         make_identity(nc, ident[:])

@@ -48,7 +48,7 @@ def tile_attend_slotattn_kernel(tc, query, keys_words, keys_scales, fac, vals, o
         nc.scalar.dma_start(out=q_raw[:], in_=query.rearrange("(p j) q -> p j q", j=PACK))
 
         ks_pool = sbuf("ks_pool", [P, T], U8)
-        nc.gpsimd.memset(ks_pool[:].bitcast(I32), 0)
+        nc.vector.memset(ks_pool[:].bitcast(I32), 0)
         for r in range(4):
             nc.sync.dma_start(
                 out=ks_pool[r:P:32, :].bitcast(I32),
@@ -62,7 +62,8 @@ def tile_attend_slotattn_kernel(tc, query, keys_words, keys_scales, fac, vals, o
         )
 
         ident = sbuf("ident", [P, P], F32)
-        make_identity(nc, ident[:])
+        nc.vector.memset(ident[:], 0.0)
+        make_identity(nc, ident[:], nomemset=True)
 
         v_pool = {}
 

@@ -85,11 +85,14 @@ def tile_attend_slotattn_kernel(tc, query, keys_words, keys_scales, fac, vals, o
         nc.vector.quantize_mx(
             out=q_codes[:].bitcast(FP8X4), scales=q_scales[:], in_=q_bf[:].rearrange("p q t -> p (q t)")
         )
-        k_scales = sbuf("k_scales", [P, PACK, P], U8)
-        nc.vector.tensor_copy(k_scales[:], ks_listed[:].rearrange("p (s t) -> p t s", t=PACK))
+        ks_dealt = ks_listed[:].rearrange("p (s t) -> p t s", t=PACK)
+        k_scales_a = sbuf("k_scales_a", [P, 2, P], U8)
+        nc.vector.tensor_copy(k_scales_a[:], ks_dealt[:, 0:2, :])
         k_codes = sbuf("k_codes", [P, PACK, P], U32, "q_bf")
         nc.vector.tensor_copy(k_codes[:].rearrange("p t s -> p s t"), kw_pool[:].indirect(offsets[:]))
-        load_values(3, "kw_pool")
+        k_scales_b = sbuf("k_scales_b", [P, 2, P], U8, "kw_pool")
+        nc.vector.tensor_copy(k_scales_b[:], ks_dealt[:, 2:4, :])
+        k_scales = [k_scales_a[:, 0, :], k_scales_a[:, 1, :], k_scales_b[:, 0, :], k_scales_b[:, 1, :]]
 
         listed0 = sbuf("v_listed0", [P, I], BF16)
         words0 = listed0[:].bitcast(F32)
@@ -101,7 +104,7 @@ def tile_attend_slotattn_kernel(tc, query, keys_words, keys_scales, fac, vals, o
             nc.tensor.matmul_mx(
                 out=scores[:],
                 lhsT=k_codes[:, t, :].bitcast(FP8X4),
-                lhsT_scale=k_scales[:, t, :],
+                lhsT_scale=k_scales[t],
                 rhs=q_codes[:].bitcast(FP8X4),
                 rhs_scale=q_scales[:],
                 start=True,
@@ -115,6 +118,8 @@ def tile_attend_slotattn_kernel(tc, query, keys_words, keys_scales, fac, vals, o
                 bias=neg_max[t],
                 accum_out=row_sum[t // 2][:, t % 2 : t % 2 + 1],
             )
+
+        load_values(3, "kw_pool")
 
         def gather(c, tag):
             listed = sbuf(f"v_listed{c}", [P, I], BF16, tag)

@@ -21,6 +21,7 @@ P = 128
 PACK = 4
 BLOCKS = E // P
 HALVES = Q // P
+CUT = 320
 
 
 def interleave(copy, dst, src):
@@ -86,17 +87,18 @@ def tile_attend_slotattn_kernel(tc, query, keys_words, keys_scales, fac, vals, o
             out=q_codes[:].bitcast(FP8X4), scales=q_scales[:], in_=q_bf[:].rearrange("p q t -> p (q t)")
         )
         ks_dealt = ks_listed[:].rearrange("p (s t) -> p t s", t=PACK)
-        k_scales_a = sbuf("k_scales_a", [P, 2, P], U8)
-        nc.vector.tensor_copy(k_scales_a[:], ks_dealt[:, 0:2, :])
+        k_scales_a = sbuf("k_scales_a", [P, P], U8)
+        nc.vector.tensor_copy(k_scales_a[:], ks_dealt[:, 0, :])
         k_codes = sbuf("k_codes", [P, PACK, P], U32, "q_bf")
         nc.vector.tensor_copy(k_codes[:].rearrange("p t s -> p s t"), kw_pool[:].indirect(offsets[:]))
-        k_scales_b = sbuf("k_scales_b", [P, 2, P], U8, "kw_pool")
-        nc.vector.tensor_copy(k_scales_b[:], ks_dealt[:, 2:4, :])
-        k_scales = [k_scales_a[:, 0, :], k_scales_a[:, 1, :], k_scales_b[:, 0, :], k_scales_b[:, 1, :]]
+        k_scales_b = sbuf("k_scales_b", [P, 3, P], U8, "kw_pool")
+        nc.vector.tensor_copy(k_scales_b[:, 0, :], ks_dealt[:, 1, :])
+        nc.vector.tensor_copy(k_scales_b[:, 1:3, :], ks_dealt[:, 2:4, :])
+        k_scales = [k_scales_a[:], k_scales_b[:, 0, :], k_scales_b[:, 1, :], k_scales_b[:, 2, :]]
 
         listed0 = sbuf("v_listed0", [P, I], BF16)
         words0 = listed0[:].bitcast(F32)
-        neg_max = [words0[:, (t // 2) * P + t % 2 : (t // 2) * P + t % 2 + 1] for t in range(PACK)]
+        neg_max = [words0[:, (t // 2) * (CUT // 2) + t % 2 : (t // 2) * (CUT // 2) + t % 2 + 1] for t in range(PACK)]
         row_sum = [sbuf(f"row_sum{u}", [P, 2], F32) for u in range(2)]
         probs = sbuf("probs", [P, PACK, Q], F32)
         for t in range(PACK):
@@ -145,16 +147,9 @@ def tile_attend_slotattn_kernel(tc, query, keys_words, keys_scales, fac, vals, o
         w_rows = sbuf("w_rows", [P, PACK, Q], BF16)
         inv_sum = [sbuf(f"inv_sum{u}", [P, 2], F32) for u in range(2)]
 
-        def gather_half(u):
-            nc.vector.tensor_copy(
-                listed0[:, u * (I // 2) : (u + 1) * (I // 2)],
-                v_pool[0][:].indirect(offsets[:, u * (I // 32) : (u + 1) * (I // 32)]),
-            )
-
-        nc.vector.reciprocal(out=inv_sum[0][:], in_=row_sum[0][:])
-        gather_half(0)
-        nc.vector.reciprocal(out=inv_sum[1][:], in_=row_sum[1][:])
-        for u in range(2):
+        for u, (first, last) in enumerate(((0, CUT), (CUT, I))):
+            nc.vector.reciprocal(out=inv_sum[u][:], in_=row_sum[u][:])
+            nc.vector.tensor_copy(listed0[:, first:last], v_pool[0][:].indirect(offsets[:, first // 16 : last // 16]))
             row_factor = sbuf(f"row_factor{u}", [P, 2], F32)
             nc.vector.tensor_tensor(
                 out=row_factor[:], in0=inv_sum[u][:], in1=fac_sb[:, 2 * u : 2 * u + 2], op=ALU.mult
@@ -166,7 +161,6 @@ def tile_attend_slotattn_kernel(tc, query, keys_words, keys_scales, fac, vals, o
                     func=ACT.Copy,
                     scale=row_factor[:, b : b + 1],
                 )
-        gather_half(1)
         wv_bf = sbuf("wv_bf", [P, Q + 2 * P, PACK], BF16)
         turn(listed0, wv_bf[:, Q : Q + P, :])
         interleave(nc.scalar.copy, wv_bf[:, 0:Q, :], w_rows[:])
@@ -175,9 +169,16 @@ def tile_attend_slotattn_kernel(tc, query, keys_words, keys_scales, fac, vals, o
         listed2 = gather(2, "inv_sum1")
         vt2 = sbuf("vt2", [P, P, PACK], BF16)
         turn(listed2, vt2[:])
-        wv_codes, wv_scales = quantize("wv", "ks_pool", wv_bf[:])
+        wv_codes = sbuf("wv_codes", [P, Q + 2 * P], U32, "ks_pool")
+        wv_scales = sbuf("wv_scales", [P, Q + 2 * P], U8)
         w_codes, w_scales = wv_codes[:, 0:Q], wv_scales[:, 0:Q]
         v01 = wv_codes[:, Q : Q + 2 * P], wv_scales[:, Q : Q + 2 * P]
+        for cols in (slice(0, Q), slice(Q, Q + 2 * P)):
+            nc.vector.quantize_mx(
+                out=wv_codes[:, cols].bitcast(FP8X4),
+                scales=wv_scales[:, cols],
+                in_=wv_bf[:, cols, :].rearrange("p e t -> p (e t)"),
+            )
 
         out_rows = out.rearrange("(h p) e -> p h e", p=P)
 

@@ -98,7 +98,8 @@ def tile_attend_slotattn_kernel(tc, query, keys_words, keys_scales, fac, vals, o
 
         listed0 = sbuf("v_listed0", [P, I], BF16)
         words0 = listed0[:].bitcast(F32)
-        neg_max = [words0[:, (t // 2) * (CUT // 2) + t % 2 : (t // 2) * (CUT // 2) + t % 2 + 1] for t in range(PACK)]
+        neg_max2 = sbuf("neg_max2", [P, 1], F32, "row_factor0")
+        neg_max = [words0[:, 0:1], words0[:, 1:2], neg_max2[:], words0[:, CUT // 2 : CUT // 2 + 1]]
         row_sum = [sbuf(f"row_sum{u}", [P, 2], F32) for u in range(2)]
         probs = sbuf("probs", [P, PACK, Q], F32)
         for t in range(PACK):

@@ -205,6 +205,8 @@ def tile_attend_slotattn_kernel(tc, query, keys_words, keys_scales, fac, vals, o
             nc.sync.dma_start(out=out_rows[:, :, first : first + width], in_=result[:])
 
         both_halves("first", v01, 0, "bank0")
+        warm = psum.tile([P, Q + 2 * P], F32, name="warm")
+        product(warm[:], 0, (wv_codes[:], wv_scales[:]))
         listed3 = gather(3, None)
         vt3 = sbuf("vt3", [P, P, PACK], BF16)
         turn(listed3, vt3[:])

@@ -207,9 +207,13 @@ def tile_attend_slotattn_kernel(tc, query, keys_words, keys_scales, fac, vals, o
         both_halves("first", v01, 0, "bank0")
         warm = psum.tile([P, Q + 2 * P], F32, name="warm")
         product(warm[:], 0, (wv_codes[:], wv_scales[:]))
-        listed3 = gather(3, None)
+        listed3 = sbuf("v_listed3", [P, 2, P, 2], BF16)
+        nc.vector.tensor_copy(listed3[:].rearrange("p u s b -> p s u b"), v_pool[3][:].indirect(offsets[:]))
         vt3 = sbuf("vt3", [P, P, PACK], BF16)
-        turn(listed3, vt3[:])
+        turned3 = psum.tile([P, 2, P], F32, name="turned3", tag="turned", bufs=2)
+        for u in range(2):
+            nc.tensor.transpose(turned3[:, u, :], listed3[:, u].rearrange("p s b -> p (s b)").bitcast(F32), ident[:])
+        nc.scalar.copy(out=vt3[:].bitcast(F32), in_=turned3[:].rearrange("p u e -> p e u"))
         v2 = quantize("v2", "kw_pool", vt2[:])
         both_halves("middle", v2, 2 * P, "bank1")
         v3 = quantize("v3", None, vt3[:])

@@ -19,25 +19,21 @@ AX = mybir.AxisListType
 
 P = 128
 PACK = 4
-BLOCKS = E // P
 HALVES = Q // P
+SHARE = 256
 CUT = 320
-
-
-def interleave(copy, dst, src):
-    copy(
-        out=dst.rearrange("p (c i) t -> p c t i", i=4),
-        in_=src.rearrange("p t (c i) -> p c t i", i=4),
-    )
 
 
 def tile_attend_slotattn_kernel(tc, query, keys_words, keys_scales, fac, vals, offs, out):
     nc = tc.nc
     with ExitStack() as ctx:
         keep = ctx.enter_context(tc.tile_pool(name="keep", bufs=1))
+        turns = ctx.enter_context(tc.tile_pool(name="turns", bufs=1))
         psum = ctx.enter_context(tc.psum_pool(name="psum", bufs=1))
 
-        def sbuf(name, shape, dtype, tag=None):
+        def sbuf(name, shape, dtype, tag=None, at=None):
+            if at is not None:
+                return turns.tile(shape, dtype, name=name, tag=name, align_bytes=64, offset=at)
             return keep.tile(shape, dtype, name=name, tag=tag or name, align_bytes=64)
 
         offsets = keep.tile([P, I // 16], U16, name="offsets")
@@ -48,7 +44,7 @@ def tile_attend_slotattn_kernel(tc, query, keys_words, keys_scales, fac, vals, o
         q_raw = sbuf("q_raw", [P, PACK, Q], F32)
         nc.scalar.dma_start(out=q_raw[:], in_=query.rearrange("(p j) q -> p j q", j=PACK))
 
-        ks_pool = sbuf("ks_pool", [P, T], U8)
+        ks_pool = sbuf("ks_pool", [P, T], U8, at=8192)
         nc.vector.memset(ks_pool[:].bitcast(I32), 0)
         for r in range(4):
             nc.sync.dma_start(
@@ -56,7 +52,7 @@ def tile_attend_slotattn_kernel(tc, query, keys_words, keys_scales, fac, vals, o
                 in_=keys_scales[0, r:16:4, :].bitcast(I32),
             )
 
-        kw_pool = sbuf("kw_pool", [P, T], U32)
+        kw_pool = sbuf("kw_pool", [P, T], U32, at=0)
         nc.sync.dma_start(
             out=kw_pool[:].bitcast(I32),
             in_=keys_words[0].rearrange("p n t -> p (n t)").bitcast(I32),
@@ -68,46 +64,43 @@ def tile_attend_slotattn_kernel(tc, query, keys_words, keys_scales, fac, vals, o
 
         v_pool = {}
 
-        def load_values(c, tag):
-            v_pool[c] = sbuf(f"v_pool{c}", [P, T], F32, tag)
+        def load_values(c, tag, at=None):
+            v_pool[c] = sbuf(f"v_pool{c}", [P, T], F32, tag, at)
             nc.sync.dma_start(out=v_pool[c][:], in_=vals[c * P : (c + 1) * P, :])
 
         load_values(0, None)
 
         q_bf = sbuf("q_bf", [P, Q, PACK], BF16)
-        interleave(nc.scalar.copy, q_bf[:], q_raw[:])
+        nc.scalar.copy(
+            out=q_bf[:].rearrange("p (c i) t -> p c t i", i=4),
+            in_=q_raw[:].rearrange("p t (c i) -> p c t i", i=4),
+        )
         load_values(1, "q_raw")
 
-        ks_listed = sbuf("ks_listed", [P, I], U8)
-        nc.vector.tensor_copy(ks_listed[:], ks_pool[:].indirect(offsets[:]))
-        load_values(2, "ks_pool")
+        k_scales = sbuf("k_scales", [P, PACK, P], U8)
+        nc.vector.tensor_copy(k_scales[:].rearrange("p t s -> p s t"), ks_pool[:].indirect(offsets[:]))
         q_codes = sbuf("q_codes", [P, Q], U32)
         q_scales = sbuf("q_scales", [P, Q], U8)
         nc.vector.quantize_mx(
             out=q_codes[:].bitcast(FP8X4), scales=q_scales[:], in_=q_bf[:].rearrange("p q t -> p (q t)")
         )
-        ks_dealt = ks_listed[:].rearrange("p (s t) -> p t s", t=PACK)
-        k_scales_a = sbuf("k_scales_a", [P, P], U8)
-        nc.vector.tensor_copy(k_scales_a[:], ks_dealt[:, 0, :])
+        load_values(2, None, 8192)
         k_codes = sbuf("k_codes", [P, PACK, P], U32, "q_bf")
         nc.vector.tensor_copy(k_codes[:].rearrange("p t s -> p s t"), kw_pool[:].indirect(offsets[:]))
-        k_scales_b = sbuf("k_scales_b", [P, 3, P], U8, "kw_pool")
-        nc.vector.tensor_copy(k_scales_b[:, 0, :], ks_dealt[:, 1, :])
-        nc.vector.tensor_copy(k_scales_b[:, 1:3, :], ks_dealt[:, 2:4, :])
-        k_scales = [k_scales_a[:], k_scales_b[:, 0, :], k_scales_b[:, 1, :], k_scales_b[:, 2, :]]
+        load_values(3, None, 0)
 
         listed0 = sbuf("v_listed0", [P, I], BF16)
         words0 = listed0[:].bitcast(F32)
-        neg_max2 = sbuf("neg_max2", [P, 1], F32, "row_factor0")
+        neg_max2 = sbuf("neg_max2", [P, 1], F32)
         neg_max = [words0[:, 0:1], words0[:, 1:2], neg_max2[:], words0[:, CUT // 2 : CUT // 2 + 1]]
-        row_sum = [sbuf(f"row_sum{u}", [P, 2], F32) for u in range(2)]
+        row_sum = sbuf("row_sum", [P, PACK], F32)
         probs = sbuf("probs", [P, PACK, Q], F32)
         for t in range(PACK):
             scores = psum.tile([P, Q], F32, name=f"scores{t}", tag=f"bank{t}")
             nc.tensor.matmul_mx(
                 out=scores[:],
                 lhsT=k_codes[:, t, :].bitcast(FP8X4),
-                lhsT_scale=k_scales[t],
+                lhsT_scale=k_scales[:, t, :],
                 rhs=q_codes[:].bitcast(FP8X4),
                 rhs_scale=q_scales[:],
                 start=True,
@@ -119,14 +112,15 @@ def tile_attend_slotattn_kernel(tc, query, keys_words, keys_scales, fac, vals, o
                 in_=scores[:],
                 func=ACT.Exp,
                 bias=neg_max[t],
-                accum_out=row_sum[t // 2][:, t % 2 : t % 2 + 1],
+                accum_out=row_sum[:, t : t + 1],
             )
 
-        load_values(3, "kw_pool")
-
-        def gather(c, tag):
+        def gather(c, share, tag=None):
             listed = sbuf(f"v_listed{c}", [P, I], BF16, tag)
-            nc.vector.tensor_copy(listed[:], v_pool[c][:].indirect(offsets[:]))
+            if share > 0:
+                nc.vector.tensor_copy(listed[:, 0:share], v_pool[c][:].indirect(offsets[:, 0 : share // 16]))
+            if share < I:
+                nc.scalar.activation(listed[:, share:I], v_pool[c][:].indirect(offsets[:, share // 16 : I // 16]), ACT.Copy)
             return listed
 
         def turn(listed, vt_bf):
@@ -136,50 +130,35 @@ def tile_attend_slotattn_kernel(tc, query, keys_words, keys_scales, fac, vals, o
                 nc.tensor.transpose(turned[:, u, :], pairs[:, u : I // 2 : 2], ident[:])
             nc.scalar.copy(out=vt_bf.bitcast(F32), in_=turned[:].rearrange("p u e -> p e u"))
 
-        def quantize(name, tag, values):
+        def quantize(name, values, at=None):
             width = values.shape[1]
-            codes = sbuf(name + "_codes", [P, width], U32, tag)
+            codes = sbuf(name + "_codes", [P, width], U32, None, at)
             scales = sbuf(name + "_scales", [P, width], U8)
             nc.vector.quantize_mx(
                 out=codes[:].bitcast(FP8X4), scales=scales[:], in_=values.rearrange("p e t -> p (e t)")
             )
             return codes[:], scales[:]
 
-        w_rows = sbuf("w_rows", [P, PACK, Q], BF16)
-        inv_sum = [sbuf(f"inv_sum{u}", [P, 2], F32) for u in range(2)]
-
-        for u, (first, last) in enumerate(((0, CUT), (CUT, I))):
-            nc.vector.reciprocal(out=inv_sum[u][:], in_=row_sum[u][:])
-            nc.vector.tensor_copy(listed0[:, first:last], v_pool[0][:].indirect(offsets[:, first // 16 : last // 16]))
-            row_factor = sbuf(f"row_factor{u}", [P, 2], F32)
-            nc.vector.tensor_tensor(
-                out=row_factor[:], in0=inv_sum[u][:], in1=fac_sb[:, 2 * u : 2 * u + 2], op=ALU.mult
-            )
-            for b in range(2):
-                nc.scalar.activation(
-                    out=w_rows[:, 2 * u + b, :],
-                    in_=probs[:, 2 * u + b, :],
-                    func=ACT.Copy,
-                    scale=row_factor[:, b : b + 1],
-                )
-        wv_bf = sbuf("wv_bf", [P, Q + 2 * P, PACK], BF16)
-        turn(listed0, wv_bf[:, Q : Q + P, :])
-        interleave(nc.scalar.copy, wv_bf[:, 0:Q, :], w_rows[:])
-        listed1 = gather(1, "row_sum1")
-        turn(listed1, wv_bf[:, Q + P : Q + 2 * P, :])
-        listed2 = gather(2, "inv_sum1")
-        vt2 = sbuf("vt2", [P, P, PACK], BF16)
-        turn(listed2, vt2[:])
-        wv_codes = sbuf("wv_codes", [P, Q + 2 * P], U32, "ks_pool")
-        wv_scales = sbuf("wv_scales", [P, Q + 2 * P], U8)
-        w_codes, w_scales = wv_codes[:, 0:Q], wv_scales[:, 0:Q]
-        v01 = wv_codes[:, Q : Q + 2 * P], wv_scales[:, Q : Q + 2 * P]
-        for cols in (slice(0, Q), slice(Q, Q + 2 * P)):
-            nc.vector.quantize_mx(
-                out=wv_codes[:, cols].bitcast(FP8X4),
-                scales=wv_scales[:, cols],
-                in_=wv_bf[:, cols, :].rearrange("p e t -> p (e t)"),
-            )
+        nc.vector.tensor_copy(listed0[:, 0:CUT], v_pool[0][:].indirect(offsets[:, 0 : CUT // 16]))
+        inv_sum = sbuf("inv_sum", [P, PACK], F32)
+        nc.vector.reciprocal(out=inv_sum[:], in_=row_sum[:])
+        nc.vector.tensor_copy(listed0[:, CUT:I], v_pool[0][:].indirect(offsets[:, CUT // 16 : I // 16]))
+        row_factor = sbuf("row_factor", [P, PACK], F32)
+        nc.vector.tensor_tensor(out=row_factor[:], in0=inv_sum[:], in1=fac_sb[:], op=ALU.mult)
+        w_bf = sbuf("w_bf", [P, Q, PACK], BF16)
+        nc.vector.tensor_tensor(
+            out=w_bf[:].rearrange("p (c i) t -> p c t i", i=4),
+            in0=probs[:].rearrange("p t (c i) -> p c t i", i=4),
+            in1=row_factor[:].unsqueeze(1).unsqueeze(3).to_broadcast([P, Q // 4, PACK, 4]),
+            op=ALU.mult,
+        )
+        listed1 = gather(1, 0)
+        vt01 = sbuf("vt01", [P, 2 * P, PACK], BF16, "q_raw")
+        turn(listed0, vt01[:, 0:P, :])
+        turn(listed1, vt01[:, P : 2 * P, :])
+        listed2 = gather(2, SHARE)
+        w_codes, w_scales = quantize("w", w_bf[:], 8192)
+        v01 = quantize("v01", vt01[:], 8192 + 1024)
 
         out_rows = out.rearrange("(h p) e -> p h e", p=P)
 
@@ -195,28 +174,24 @@ def tile_attend_slotattn_kernel(tc, query, keys_words, keys_scales, fac, vals, o
                 stop=True,
             )
 
-        def both_halves(name, values, first, bank):
+        def both_halves(name, values, first, bank, copy, at=None):
             width = values[0].shape[1]
             acc = psum.tile([P, HALVES, width], F32, name=name + "_acc", tag=bank)
             for h in range(HALVES):
                 product(acc[:, h, :], h, values)
-            result = sbuf(name + "_out", [P, HALVES, width], F32)
-            nc.scalar.copy(out=result[:], in_=acc[:])
+            result = sbuf(name + "_out", [P, HALVES, width], F32, None, at)
+            copy(out=result[:], in_=acc[:])
             nc.sync.dma_start(out=out_rows[:, :, first : first + width], in_=result[:])
 
-        both_halves("first", v01, 0, "bank0")
-        warm = psum.tile([P, Q + 2 * P], F32, name="warm")
-        product(warm[:], 0, (wv_codes[:], wv_scales[:]))
-        listed3 = sbuf("v_listed3", [P, 2, P, 2], BF16)
-        nc.vector.tensor_copy(listed3[:].rearrange("p u s b -> p s u b"), v_pool[3][:].indirect(offsets[:]))
+        vt2 = sbuf("vt2", [P, P, PACK], BF16)
+        turn(listed2, vt2[:])
+        listed3 = gather(3, SHARE)
+        v2 = quantize("v2", vt2[:], 0)
+        both_halves("first", v01, 0, "bank0", nc.vector.tensor_copy, 1024)
         vt3 = sbuf("vt3", [P, P, PACK], BF16)
-        turned3 = psum.tile([P, 2, P], F32, name="turned3", tag="turned", bufs=2)
-        for u in range(2):
-            nc.tensor.transpose(turned3[:, u, :], listed3[:, u].rearrange("p s b -> p (s b)").bitcast(F32), ident[:])
-        nc.scalar.copy(out=vt3[:].bitcast(F32), in_=turned3[:].rearrange("p u e -> p e u"))
-        v2 = quantize("v2", "kw_pool", vt2[:])
-        both_halves("middle", v2, 2 * P, "bank1")
-        v3 = quantize("v3", None, vt3[:])
+        turn(listed3, vt3[:])
+        both_halves("middle", v2, 2 * P, "bank1", nc.scalar.copy)
+        v3 = quantize("v3", vt3[:])
         for h, (copy, queue) in enumerate(((nc.vector.tensor_copy, nc.sync), (nc.scalar.copy, nc.scalar))):
             acc_h = psum.tile([P, P], F32, name=f"acc_last{h}", tag=f"bank{2 + h}")
             product(acc_h[:], h, v3)

@@ -20,8 +20,16 @@ AX = mybir.AxisListType
 P = 128
 PACK = 4
 HALVES = Q // P
-SHARE = 256
+WINDOW = 4 * T
 CUT = 320
+SHARES = (0, 0, 256, 256)
+
+
+def interleave(copy, dst, src):
+    copy(
+        out=dst.rearrange("p (c i) t -> p c t i", i=4),
+        in_=src.rearrange("p t (c i) -> p c t i", i=4),
+    )
 
 
 def tile_attend_slotattn_kernel(tc, query, keys_words, keys_scales, fac, vals, offs, out):
@@ -31,20 +39,23 @@ def tile_attend_slotattn_kernel(tc, query, keys_words, keys_scales, fac, vals, o
         turns = ctx.enter_context(tc.tile_pool(name="turns", bufs=1))
         psum = ctx.enter_context(tc.psum_pool(name="psum", bufs=1))
 
-        def sbuf(name, shape, dtype, tag=None, at=None):
-            if at is not None:
-                return turns.tile(shape, dtype, name=name, tag=name, align_bytes=64, offset=at)
-            return keep.tile(shape, dtype, name=name, tag=tag or name, align_bytes=64)
+        def sbuf(name, shape, dtype, at=None):
+            if at is None:
+                return keep.tile(shape, dtype, name=name, align_bytes=64)
+            return turns.tile(shape, dtype, name=name, align_bytes=64, offset=at)
+
+        def bank(name, shape, number):
+            return psum.tile(shape, F32, name=name, tag=f"bank{number}")
 
         offsets = keep.tile([P, I // 16], U16, name="offsets")
         nc.sync.dma_start(offsets[:], offs)
         fac_sb = sbuf("fac_sb", [P, PACK], F32)
         nc.sync.dma_start(out=fac_sb[:], in_=fac.rearrange("(p t) o -> p (t o)", t=PACK))
 
-        q_raw = sbuf("q_raw", [P, PACK, Q], F32)
+        q_raw = sbuf("q_raw", [P, PACK, Q], F32, 1 * WINDOW)
         nc.scalar.dma_start(out=q_raw[:], in_=query.rearrange("(p j) q -> p j q", j=PACK))
 
-        ks_pool = sbuf("ks_pool", [P, T], U8, at=8192)
+        ks_pool = sbuf("ks_pool", [P, T], U8, 2 * WINDOW)
         nc.vector.memset(ks_pool[:].bitcast(I32), 0)
         for r in range(4):
             nc.sync.dma_start(
@@ -52,42 +63,62 @@ def tile_attend_slotattn_kernel(tc, query, keys_words, keys_scales, fac, vals, o
                 in_=keys_scales[0, r:16:4, :].bitcast(I32),
             )
 
-        kw_pool = sbuf("kw_pool", [P, T], U32, at=0)
+        kw_pool = sbuf("kw_pool", [P, T], U32, 3 * WINDOW)
         nc.sync.dma_start(
             out=kw_pool[:].bitcast(I32),
             in_=keys_words[0].rearrange("p n t -> p (n t)").bitcast(I32),
         )
 
+        k_scales = sbuf("k_scales", [P, PACK, P], U8)
         ident = sbuf("ident", [P, P], F32)
         nc.vector.memset(ident[:], 0.0)
         make_identity(nc, ident[:], nomemset=True)
 
         v_pool = {}
 
-        def load_values(c, tag, at=None):
-            v_pool[c] = sbuf(f"v_pool{c}", [P, T], F32, tag, at)
+        def load_values(c):
+            v_pool[c] = sbuf(f"v_pool{c}", [P, T], F32, c * WINDOW)
             nc.sync.dma_start(out=v_pool[c][:], in_=vals[c * P : (c + 1) * P, :])
 
-        load_values(0, None)
+        load_values(0)
 
         q_bf = sbuf("q_bf", [P, Q, PACK], BF16)
-        nc.scalar.copy(
-            out=q_bf[:].rearrange("p (c i) t -> p c t i", i=4),
-            in_=q_raw[:].rearrange("p t (c i) -> p c t i", i=4),
-        )
-        load_values(1, "q_raw")
-
-        k_scales = sbuf("k_scales", [P, PACK, P], U8)
+        interleave(nc.scalar.copy, q_bf[:], q_raw[:])
         nc.vector.tensor_copy(k_scales[:].rearrange("p t s -> p s t"), ks_pool[:].indirect(offsets[:]))
         q_codes = sbuf("q_codes", [P, Q], U32)
         q_scales = sbuf("q_scales", [P, Q], U8)
         nc.vector.quantize_mx(
             out=q_codes[:].bitcast(FP8X4), scales=q_scales[:], in_=q_bf[:].rearrange("p q t -> p (q t)")
         )
-        load_values(2, None, 8192)
-        k_codes = sbuf("k_codes", [P, PACK, P], U32, "q_bf")
+        load_values(1)
+        load_values(2)
+        k_codes = sbuf("k_codes", [P, PACK, P], U32)
         nc.vector.tensor_copy(k_codes[:].rearrange("p t s -> p s t"), kw_pool[:].indirect(offsets[:]))
-        load_values(3, None, 0)
+        load_values(3)
+
+        def gather(c):
+            share = SHARES[c]
+            listed = sbuf(f"v_listed{c}", [P, I], BF16)
+            if share > 0:
+                nc.vector.tensor_copy(listed[:, 0:share], v_pool[c][:].indirect(offsets[:, 0 : share // 16]))
+            nc.scalar.activation(listed[:, share:I], v_pool[c][:].indirect(offsets[:, share // 16 : I // 16]), ACT.Copy)
+            return listed
+
+        def turn(listed, vt_bf, number, copy):
+            pairs = listed[:].bitcast(F32)
+            turned = bank(f"turned{number}", [P, 2, P], number)
+            for u in range(2):
+                nc.tensor.transpose(turned[:, u, :], pairs[:, u : I // 2 : 2], ident[:])
+            copy(out=vt_bf.bitcast(F32), in_=turned[:].rearrange("p u e -> p e u"))
+
+        def quantize(name, values, at=None):
+            width = values.shape[1]
+            codes = sbuf(name + "_codes", [P, width], U32, at)
+            scales = sbuf(name + "_scales", [P, width], U8)
+            nc.vector.quantize_mx(
+                out=codes[:].bitcast(FP8X4), scales=scales[:], in_=values.rearrange("p e t -> p (e t)")
+            )
+            return codes[:], scales[:]
 
         listed0 = sbuf("v_listed0", [P, I], BF16)
         words0 = listed0[:].bitcast(F32)
@@ -96,7 +127,7 @@ def tile_attend_slotattn_kernel(tc, query, keys_words, keys_scales, fac, vals, o
         row_sum = sbuf("row_sum", [P, PACK], F32)
         probs = sbuf("probs", [P, PACK, Q], F32)
         for t in range(PACK):
-            scores = psum.tile([P, Q], F32, name=f"scores{t}", tag=f"bank{t}")
+            scores = bank(f"scores{t}", [P, Q], t)
             nc.tensor.matmul_mx(
                 out=scores[:],
                 lhsT=k_codes[:, t, :].bitcast(FP8X4),
@@ -115,30 +146,6 @@ def tile_attend_slotattn_kernel(tc, query, keys_words, keys_scales, fac, vals, o
                 accum_out=row_sum[:, t : t + 1],
             )
 
-        def gather(c, share, tag=None):
-            listed = sbuf(f"v_listed{c}", [P, I], BF16, tag)
-            if share > 0:
-                nc.vector.tensor_copy(listed[:, 0:share], v_pool[c][:].indirect(offsets[:, 0 : share // 16]))
-            if share < I:
-                nc.scalar.activation(listed[:, share:I], v_pool[c][:].indirect(offsets[:, share // 16 : I // 16]), ACT.Copy)
-            return listed
-
-        def turn(listed, vt_bf):
-            pairs = listed[:].bitcast(F32)
-            turned = psum.tile([P, 2, P], F32, name="turned", tag="turned", bufs=2)
-            for u in range(2):
-                nc.tensor.transpose(turned[:, u, :], pairs[:, u : I // 2 : 2], ident[:])
-            nc.scalar.copy(out=vt_bf.bitcast(F32), in_=turned[:].rearrange("p u e -> p e u"))
-
-        def quantize(name, values, at=None):
-            width = values.shape[1]
-            codes = sbuf(name + "_codes", [P, width], U32, None, at)
-            scales = sbuf(name + "_scales", [P, width], U8)
-            nc.vector.quantize_mx(
-                out=codes[:].bitcast(FP8X4), scales=scales[:], in_=values.rearrange("p e t -> p (e t)")
-            )
-            return codes[:], scales[:]
-
         nc.vector.tensor_copy(listed0[:, 0:CUT], v_pool[0][:].indirect(offsets[:, 0 : CUT // 16]))
         inv_sum = sbuf("inv_sum", [P, PACK], F32)
         nc.vector.reciprocal(out=inv_sum[:], in_=row_sum[:])
@@ -152,13 +159,24 @@ def tile_attend_slotattn_kernel(tc, query, keys_words, keys_scales, fac, vals, o
             in1=row_factor[:].unsqueeze(1).unsqueeze(3).to_broadcast([P, Q // 4, PACK, 4]),
             op=ALU.mult,
         )
-        listed1 = gather(1, 0)
-        vt01 = sbuf("vt01", [P, 2 * P, PACK], BF16, "q_raw")
-        turn(listed0, vt01[:, 0:P, :])
-        turn(listed1, vt01[:, P : 2 * P, :])
-        listed2 = gather(2, SHARE)
-        w_codes, w_scales = quantize("w", w_bf[:], 8192)
-        v01 = quantize("v01", vt01[:], 8192 + 1024)
+        listed1 = gather(1)
+        vt0 = sbuf("vt0", [P, P, PACK], BF16, 1 * WINDOW)
+        turn(listed0, vt0[:], 0, nc.scalar.copy)
+        listed2 = gather(2)
+        vt1 = sbuf("vt1", [P, P, PACK], BF16, 2 * WINDOW + 1024)
+        turn(listed1, vt1[:], 1, nc.scalar.copy)
+        w_codes, w_scales = quantize("w", w_bf[:], 2 * WINDOW)
+        v01_codes = sbuf("v01_codes", [P, 2 * P], U32, 2 * WINDOW + 2048)
+        v01_scales = sbuf("v01_scales", [P, 2 * P], U8)
+        v01 = v01_codes[:], v01_scales[:]
+        for c, values in enumerate((vt0, vt1)):
+            nc.vector.quantize_mx(
+                out=v01_codes[:, c * P : (c + 1) * P].bitcast(FP8X4),
+                scales=v01_scales[:, c * P : (c + 1) * P],
+                in_=values[:].rearrange("p e t -> p (e t)"),
+            )
+        vt2 = sbuf("vt2", [P, P, PACK], BF16)
+        turn(listed2, vt2[:], 4, nc.scalar.copy)
 
         out_rows = out.rearrange("(h p) e -> p h e", p=P)
 
@@ -174,26 +192,24 @@ def tile_attend_slotattn_kernel(tc, query, keys_words, keys_scales, fac, vals, o
                 stop=True,
             )
 
-        def both_halves(name, values, first, bank, copy, at=None):
+        def both_halves(name, values, first, number, copy, at=None):
             width = values[0].shape[1]
-            acc = psum.tile([P, HALVES, width], F32, name=name + "_acc", tag=bank)
+            acc = bank(name + "_acc", [P, HALVES, width], number)
             for h in range(HALVES):
                 product(acc[:, h, :], h, values)
-            result = sbuf(name + "_out", [P, HALVES, width], F32, None, at)
+            result = sbuf(name + "_out", [P, HALVES, width], F32, at)
             copy(out=result[:], in_=acc[:])
             nc.sync.dma_start(out=out_rows[:, :, first : first + width], in_=result[:])
 
-        vt2 = sbuf("vt2", [P, P, PACK], BF16)
-        turn(listed2, vt2[:])
-        listed3 = gather(3, SHARE)
-        v2 = quantize("v2", vt2[:], 0)
-        both_halves("first", v01, 0, "bank0", nc.vector.tensor_copy, 1024)
+        listed3 = gather(3)
+        v2 = quantize("v2", vt2[:], 3 * WINDOW)
+        both_halves("first", v01, 0, 2, nc.vector.tensor_copy, 3 * WINDOW + 1024)
         vt3 = sbuf("vt3", [P, P, PACK], BF16)
-        turn(listed3, vt3[:])
-        both_halves("middle", v2, 2 * P, "bank1", nc.scalar.copy)
+        turn(listed3, vt3[:], 5, nc.scalar.copy)
+        both_halves("middle", v2, 2 * P, 3, nc.scalar.copy)
         v3 = quantize("v3", vt3[:])
         for h, (copy, queue) in enumerate(((nc.vector.tensor_copy, nc.sync), (nc.scalar.copy, nc.scalar))):
-            acc_h = psum.tile([P, P], F32, name=f"acc_last{h}", tag=f"bank{2 + h}")
+            acc_h = bank(f"acc_last{h}", [P, P], 6 + h)
             product(acc_h[:], h, v3)
             late_out = sbuf(f"late_out{h}", [P, P], F32)
             copy(out=late_out[:], in_=acc_h[:])

@@ -21,8 +21,12 @@ P = 128
 PACK = 4
 HALVES = Q // P
 WINDOW = 4 * T
-CUT = 320
-SHARES = (0, 0, 256, 256)
+NARROW = 64
+NARROW_ROWS = slice(32, 96)
+EVEN_SHARE = I // 2
+A_SHARE = 64
+B_SHARE = 224
+C_SHARE = 224
 
 
 def interleave(copy, dst, src):
@@ -74,58 +78,64 @@ def tile_attend_slotattn_kernel(tc, query, keys_words, keys_scales, fac, vals, o
         nc.vector.memset(ident[:], 0.0)
         make_identity(nc, ident[:], nomemset=True)
 
-        v_pool = {}
+        narrow_pool = sbuf("narrow_pool", [P, T], F32, 0)
+        nc.vector.memset(narrow_pool[:], 0.0)
+        nc.sync.dma_start(out=narrow_pool[NARROW_ROWS, :], in_=vals[0:NARROW, :])
 
-        def load_values(c):
-            v_pool[c] = sbuf(f"v_pool{c}", [P, T], F32, c * WINDOW)
-            nc.sync.dma_start(out=v_pool[c][:], in_=vals[c * P : (c + 1) * P, :])
+        def load_wide(c):
+            pool = sbuf(f"wide_pool{c}", [P, T], F32, (c + 1) * WINDOW)
+            nc.sync.dma_start(out=pool[:], in_=vals[NARROW + c * P : NARROW + (c + 1) * P, :])
+            return pool
 
-        load_values(0)
+        def gather(on_vector, listed, pool, lo, hi):
+            window = pool[:].indirect(offsets[:, lo // 16 : hi // 16])
+            if on_vector:
+                nc.vector.tensor_copy(listed[:, lo:hi], window)
+            else:
+                nc.scalar.activation(listed[:, lo:hi], window, ACT.Copy)
+
+        def gather_shared(name, pool, share):
+            listed = sbuf(name, [P, I], BF16)
+            gather(True, listed, pool, 0, share)
+            gather(False, listed, pool, share, I)
+            return listed
+
+        def transposed(name, listed, number):
+            pairs = listed[:].bitcast(F32)
+            turned = bank(name, [P, 2, P], number)
+            for u in range(2):
+                nc.tensor.transpose(turned[:, u, :], pairs[:, u : I // 2 : 2], ident[:])
+            return turned
+
+        def weave(copy, vt_bf, turned):
+            copy(out=vt_bf.bitcast(F32), in_=turned.rearrange("p u e -> p e u"))
+
+        def quantize(codes, scales, values):
+            nc.vector.quantize_mx(out=codes.bitcast(FP8X4), scales=scales, in_=values.rearrange("p e t -> p (e t)"))
+
+        def mx_tiles(name, width, at=None):
+            return sbuf(name + "_codes", [P, width], U32, at), sbuf(name + "_scales", [P, width], U8)
 
         q_bf = sbuf("q_bf", [P, Q, PACK], BF16)
         interleave(nc.scalar.copy, q_bf[:], q_raw[:])
         nc.vector.tensor_copy(k_scales[:].rearrange("p t s -> p s t"), ks_pool[:].indirect(offsets[:]))
-        q_codes = sbuf("q_codes", [P, Q], U32)
-        q_scales = sbuf("q_scales", [P, Q], U8)
-        nc.vector.quantize_mx(
-            out=q_codes[:].bitcast(FP8X4), scales=q_scales[:], in_=q_bf[:].rearrange("p q t -> p (q t)")
-        )
-        load_values(1)
-        load_values(2)
+        q_codes, q_scales = mx_tiles("q", Q)
+        quantize(q_codes[:], q_scales[:], q_bf[:])
+        pool_a = load_wide(0)
+        pool_b = load_wide(1)
         k_codes = sbuf("k_codes", [P, PACK, P], U32)
         nc.vector.tensor_copy(k_codes[:].rearrange("p t s -> p s t"), kw_pool[:].indirect(offsets[:]))
-        load_values(3)
+        pool_c = load_wide(2)
+        listed_d = sbuf("listed_d", [P, I], BF16)
+        gather(False, listed_d, narrow_pool, 0, I)
 
-        def gather(c):
-            share = SHARES[c]
-            listed = sbuf(f"v_listed{c}", [P, I], BF16)
-            if share > 0:
-                nc.vector.tensor_copy(listed[:, 0:share], v_pool[c][:].indirect(offsets[:, 0 : share // 16]))
-            nc.scalar.activation(listed[:, share:I], v_pool[c][:].indirect(offsets[:, share // 16 : I // 16]), ACT.Copy)
-            return listed
-
-        def turn(listed, vt_bf, number, copy):
-            pairs = listed[:].bitcast(F32)
-            turned = bank(f"turned{number}", [P, 2, P], number)
-            for u in range(2):
-                nc.tensor.transpose(turned[:, u, :], pairs[:, u : I // 2 : 2], ident[:])
-            copy(out=vt_bf.bitcast(F32), in_=turned[:].rearrange("p u e -> p e u"))
-
-        def quantize(name, values, at=None):
-            width = values.shape[1]
-            codes = sbuf(name + "_codes", [P, width], U32, at)
-            scales = sbuf(name + "_scales", [P, width], U8)
-            nc.vector.quantize_mx(
-                out=codes[:].bitcast(FP8X4), scales=scales[:], in_=values.rearrange("p e t -> p (e t)")
-            )
-            return codes[:], scales[:]
-
-        listed0 = sbuf("v_listed0", [P, I], BF16)
-        words0 = listed0[:].bitcast(F32)
-        neg_max2 = sbuf("neg_max2", [P, 1], F32)
-        neg_max = [words0[:, 0:1], words0[:, 1:2], neg_max2[:], words0[:, CUT // 2 : CUT // 2 + 1]]
-        row_sum = sbuf("row_sum", [P, PACK], F32)
-        probs = sbuf("probs", [P, PACK, Q], F32)
+        listed_a = sbuf("listed_a", [P, I], BF16)
+        words_a = listed_a[:].bitcast(F32)
+        vt_d = sbuf("vt_d", [P, NARROW, PACK], BF16)
+        words_d = vt_d[:].rearrange("p e t -> p (e t)").bitcast(F32)
+        neg_max = [words_a[:, 0:1], words_a[:, 1:2], words_d[:, 0:1], words_a[:, I // 4 : I // 4 + 1]]
+        row_sum = sbuf("row_sum", [P, PACK], F32, 4 * WINDOW)
+        probs = sbuf("probs", [P, PACK, Q], F32, 0)
         for t in range(PACK):
             scores = bank(f"scores{t}", [P, Q], t)
             nc.tensor.matmul_mx(
@@ -146,42 +156,46 @@ def tile_attend_slotattn_kernel(tc, query, keys_words, keys_scales, fac, vals, o
                 accum_out=row_sum[:, t : t + 1],
             )
 
-        nc.vector.tensor_copy(listed0[:, 0:CUT], v_pool[0][:].indirect(offsets[:, 0 : CUT // 16]))
+        turned_d = transposed("turned_d", listed_d, 4)
+        weave(nc.vector.tensor_copy, vt_d[:], turned_d[:, :, NARROW_ROWS])
         inv_sum = sbuf("inv_sum", [P, PACK], F32)
         nc.vector.reciprocal(out=inv_sum[:], in_=row_sum[:])
-        nc.vector.tensor_copy(listed0[:, CUT:I], v_pool[0][:].indirect(offsets[:, CUT // 16 : I // 16]))
+        d_codes, d_scales = mx_tiles("d", NARROW, 4 * WINDOW)
+        quantize(d_codes[:], d_scales[:], vt_d[:])
         row_factor = sbuf("row_factor", [P, PACK], F32)
         nc.vector.tensor_tensor(out=row_factor[:], in0=inv_sum[:], in1=fac_sb[:], op=ALU.mult)
-        w_bf = sbuf("w_bf", [P, Q, PACK], BF16)
-        nc.vector.tensor_tensor(
-            out=w_bf[:].rearrange("p (c i) t -> p c t i", i=4),
-            in0=probs[:].rearrange("p t (c i) -> p c t i", i=4),
-            in1=row_factor[:].unsqueeze(1).unsqueeze(3).to_broadcast([P, Q // 4, PACK, 4]),
-            op=ALU.mult,
-        )
-        listed1 = gather(1)
-        vt0 = sbuf("vt0", [P, P, PACK], BF16, 1 * WINDOW)
-        turn(listed0, vt0[:], 0, nc.scalar.copy)
-        listed2 = gather(2)
-        vt1 = sbuf("vt1", [P, P, PACK], BF16, 2 * WINDOW + 1024)
-        turn(listed1, vt1[:], 1, nc.scalar.copy)
-        w_codes, w_scales = quantize("w", w_bf[:], 2 * WINDOW)
-        v01_codes = sbuf("v01_codes", [P, 2 * P], U32, 2 * WINDOW + 2048)
-        v01_scales = sbuf("v01_scales", [P, 2 * P], U8)
-        v01 = v01_codes[:], v01_scales[:]
-        for c, values in enumerate((vt0, vt1)):
-            nc.vector.quantize_mx(
-                out=v01_codes[:, c * P : (c + 1) * P].bitcast(FP8X4),
-                scales=v01_scales[:, c * P : (c + 1) * P],
-                in_=values[:].rearrange("p e t -> p (e t)"),
+        gather(True, listed_a, pool_a, 0, A_SHARE)
+        gather(False, listed_a, pool_a, A_SHARE, I)
+        nc.sync.dma_start(out=pool_a[NARROW_ROWS, :], in_=vals[E - NARROW : E, :])
+
+        def weights(h, at):
+            w_bf = sbuf(f"w_bf{h}", [P, P, PACK], BF16, at)
+            nc.vector.tensor_tensor(
+                out=w_bf[:].rearrange("p (c i) t -> p c t i", i=4),
+                in0=probs[:, :, h * P : (h + 1) * P].rearrange("p t (c i) -> p c t i", i=4),
+                in1=row_factor[:].unsqueeze(1).unsqueeze(3).to_broadcast([P, P // 4, PACK, 4]),
+                op=ALU.mult,
             )
-        vt2 = sbuf("vt2", [P, P, PACK], BF16)
-        turn(listed2, vt2[:], 4, nc.scalar.copy)
+            return w_bf
+
+        w_low = weights(0, None)
+        turned_a = transposed("turned_a", listed_a, 5)
+        listed_b = gather_shared("listed_b", pool_b, B_SHARE)
+        w_high = weights(1, 2 * WINDOW + 2048)
+        vt_a = sbuf("vt_a", [P, P, PACK], BF16, 2 * WINDOW + 1024)
+        weave(nc.scalar.copy, vt_a[:], turned_a[:])
+        w_codes, w_scales = mx_tiles("w", Q, 2 * WINDOW)
+        for h, w_bf in enumerate((w_low, w_high)):
+            quantize(w_codes[:, h * P : (h + 1) * P], w_scales[:, h * P : (h + 1) * P], w_bf[:])
+        ab_codes, ab_scales = mx_tiles("ab", 2 * P)
+        quantize(ab_codes[:, 0:P], ab_scales[:, 0:P], vt_a[:])
+        vt_b = sbuf("vt_b", [P, P, PACK], BF16)
+        weave(nc.scalar.copy, vt_b[:], transposed("turned_b", listed_b, 0)[:])
+        quantize(ab_codes[:, P : 2 * P], ab_scales[:, P : 2 * P], vt_b[:])
 
         out_rows = out.rearrange("(h p) e -> p h e", p=P)
 
-        def product(acc, h, values):
-            v_codes, v_scales = values
+        def product(acc, h, v_codes, v_scales):
             nc.tensor.matmul_mx(
                 out=acc,
                 lhsT=w_codes[:, h * P : (h + 1) * P].bitcast(FP8X4),
@@ -192,25 +206,44 @@ def tile_attend_slotattn_kernel(tc, query, keys_words, keys_scales, fac, vals, o
                 stop=True,
             )
 
-        def both_halves(name, values, first, number, copy, at=None):
-            width = values[0].shape[1]
-            acc = bank(name + "_acc", [P, HALVES, width], number)
+        paths = ((nc.vector.tensor_copy, nc.sync), (nc.scalar.copy, nc.scalar))
+        early = NARROW + 2 * P
+        early_acc = [bank(f"early_acc{h}", [P, early], 2 + h) for h in range(HALVES)]
+        for h in range(HALVES):
+            product(early_acc[h][:, 0:NARROW], h, d_codes[:], d_scales[:])
+        for c in range(2):
             for h in range(HALVES):
-                product(acc[:, h, :], h, values)
-            result = sbuf(name + "_out", [P, HALVES, width], F32, at)
-            copy(out=result[:], in_=acc[:])
-            nc.sync.dma_start(out=out_rows[:, :, first : first + width], in_=result[:])
+                cols = slice(c * P, (c + 1) * P)
+                product(early_acc[h][:, NARROW + c * P : NARROW + (c + 1) * P], h, ab_codes[:, cols], ab_scales[:, cols])
+        listed_c = gather_shared("listed_c", pool_c, C_SHARE)
+        turned_c = transposed("turned_c", listed_c, 1)
 
-        listed3 = gather(3)
-        v2 = quantize("v2", vt2[:], 3 * WINDOW)
-        both_halves("first", v01, 0, 2, nc.vector.tensor_copy, 3 * WINDOW + 1024)
-        vt3 = sbuf("vt3", [P, P, PACK], BF16)
-        turn(listed3, vt3[:], 5, nc.scalar.copy)
-        both_halves("middle", v2, 2 * P, 3, nc.scalar.copy)
-        v3 = quantize("v3", vt3[:])
-        for h, (copy, queue) in enumerate(((nc.vector.tensor_copy, nc.sync), (nc.scalar.copy, nc.scalar))):
-            acc_h = bank(f"acc_last{h}", [P, P], 6 + h)
-            product(acc_h[:], h, v3)
-            late_out = sbuf(f"late_out{h}", [P, P], F32)
-            copy(out=late_out[:], in_=acc_h[:])
-            queue.dma_start(out=out_rows[:, h, 3 * P : 4 * P], in_=late_out[:])
+        def store_early(h):
+            early_out = sbuf(f"early_out{h}", [P, early], F32, 1 * WINDOW + (1 - h) * 4096)
+            nc.vector.tensor_copy(out=early_out[:], in_=early_acc[h][:])
+            nc.sync.dma_start(out=out_rows[:, h, 0:early], in_=early_out[:])
+
+        listed_e = gather_shared("listed_e", pool_a, EVEN_SHARE)
+        turned_e = transposed("turned_e", listed_e, 4)
+        vt_c = sbuf("vt_c", [P, P, PACK], BF16, 1 * WINDOW)
+        weave(nc.scalar.copy, vt_c[:], turned_c[:])
+        c_codes, c_scales = mx_tiles("c", P)
+        store_early(0)
+        quantize(c_codes[:], c_scales[:], vt_c[:])
+        store_early(1)
+        vt_e = sbuf("vt_e", [P, NARROW, PACK], BF16)
+        weave(nc.scalar.copy, vt_e[:], turned_e[:, :, NARROW_ROWS])
+        c_acc = bank("c_acc", [P, HALVES, P], 5)
+        for h in range(HALVES):
+            product(c_acc[:, h, :], h, c_codes[:], c_scales[:])
+        e_codes, e_scales = mx_tiles("e", NARROW)
+        quantize(e_codes[:], e_scales[:], vt_e[:])
+        c_out = sbuf("c_out", [P, HALVES, P], F32)
+        nc.scalar.copy(out=c_out[:], in_=c_acc[:])
+        nc.sync.dma_start(out=out_rows[:, :, early : early + P], in_=c_out[:])
+        for h, (copy, queue) in enumerate(paths):
+            e_acc = bank(f"e_acc{h}", [P, NARROW], 6 + h)
+            product(e_acc[:], h, e_codes[:], e_scales[:])
+            e_out = sbuf(f"e_out{h}", [P, NARROW], F32)
+            copy(out=e_out[:], in_=e_acc[:])
+            queue.dma_start(out=out_rows[:, h, E - NARROW : E], in_=e_out[:])

@@ -56,7 +56,7 @@ def tile_attend_slotattn_kernel(tc, query, keys_words, keys_scales, fac, vals, o
         fac_sb = sbuf("fac_sb", [P, PACK], F32)
         nc.sync.dma_start(out=fac_sb[:], in_=fac.rearrange("(p t) o -> p (t o)", t=PACK))
 
-        q_raw = sbuf("q_raw", [P, PACK, Q], F32, 1 * WINDOW)
+        q_raw = sbuf("q_raw", [P, PACK, Q], F32)
         nc.scalar.dma_start(out=q_raw[:], in_=query.rearrange("(p j) q -> p j q", j=PACK))
 
         ks_pool = sbuf("ks_pool", [P, T], U8, 2 * WINDOW)

@@ -220,7 +220,7 @@ def tile_attend_slotattn_kernel(tc, query, keys_words, keys_scales, fac, vals, o
 
         def store_early(h):
             early_out = sbuf(f"early_out{h}", [P, early], F32, 1 * WINDOW + (1 - h) * 4096)
-            nc.vector.tensor_copy(out=early_out[:], in_=early_acc[h][:])
+            paths[h][0](out=early_out[:], in_=early_acc[h][:])
             nc.sync.dma_start(out=out_rows[:, h, 0:early], in_=early_out[:])
 
         listed_e = gather_shared("listed_e", pool_a, EVEN_SHARE)
@@ -233,13 +233,14 @@ def tile_attend_slotattn_kernel(tc, query, keys_words, keys_scales, fac, vals, o
         store_early(1)
         vt_e = sbuf("vt_e", [P, NARROW, PACK], BF16)
         weave(nc.scalar.copy, vt_e[:], turned_e[:, :, NARROW_ROWS])
-        c_acc = bank("c_acc", [P, HALVES, P], 5)
+        c_acc = [bank(f"c_acc{h}", [P, P], 5 * h) for h in range(HALVES)]
         for h in range(HALVES):
-            product(c_acc[:, h, :], h, c_codes[:], c_scales[:])
+            product(c_acc[h][:], h, c_codes[:], c_scales[:])
         e_codes, e_scales = mx_tiles("e", NARROW)
         quantize(e_codes[:], e_scales[:], vt_e[:])
         c_out = sbuf("c_out", [P, HALVES, P], F32)
-        nc.scalar.copy(out=c_out[:], in_=c_acc[:])
+        for h in range(HALVES):
+            paths[h][0](out=c_out[:, h, :], in_=c_acc[h][:])
         nc.sync.dma_start(out=out_rows[:, :, early : early + P], in_=c_out[:])
         for h, (copy, queue) in enumerate(paths):
             e_acc = bank(f"e_acc{h}", [P, NARROW], 6 + h)

@@ -219,7 +219,7 @@ def tile_attend_slotattn_kernel(tc, query, keys_words, keys_scales, fac, vals, o
         turned_c = transposed("turned_c", listed_c, 1)
 
         def store_early(h):
-            early_out = sbuf(f"early_out{h}", [P, early], F32, 1 * WINDOW + (1 - h) * 4096)
+            early_out = sbuf(f"early_out{h}", [P, early], F32, 1 * WINDOW + (2 - h) * 2048)
             paths[h][0](out=early_out[:], in_=early_acc[h][:])
             nc.sync.dma_start(out=out_rows[:, h, 0:early], in_=early_out[:])
 

@@ -26,7 +26,7 @@ NARROW_ROWS = slice(32, 96)
 EVEN_SHARE = I // 2
 A_SHARE = 64
 B_SHARE = 224
-C_SHARE = 224
+C_SHARE = 192
 
 
 def interleave(copy, dst, src):
@@ -133,7 +133,8 @@ def tile_attend_slotattn_kernel(tc, query, keys_words, keys_scales, fac, vals, o
         words_a = listed_a[:].bitcast(F32)
         vt_d = sbuf("vt_d", [P, NARROW, PACK], BF16)
         words_d = vt_d[:].rearrange("p e t -> p (e t)").bitcast(F32)
-        neg_max = [words_a[:, 0:1], words_a[:, 1:2], words_d[:, 0:1], words_a[:, I // 4 : I // 4 + 1]]
+        last_max = sbuf("last_max", [P, 1], F32)
+        neg_max = [words_a[:, 0:1], words_a[:, I // 4 - 1 : I // 4], words_d[:, 0:1], last_max[:]]
         row_sum = sbuf("row_sum", [P, PACK], F32, 4 * WINDOW)
         probs = sbuf("probs", [P, PACK, Q], F32, 0)
         for t in range(PACK):
@@ -160,11 +161,11 @@ def tile_attend_slotattn_kernel(tc, query, keys_words, keys_scales, fac, vals, o
         weave(nc.vector.tensor_copy, vt_d[:], turned_d[:, :, NARROW_ROWS])
         inv_sum = sbuf("inv_sum", [P, PACK], F32)
         nc.vector.reciprocal(out=inv_sum[:], in_=row_sum[:])
-        d_codes, d_scales = mx_tiles("d", NARROW, 4 * WINDOW)
-        quantize(d_codes[:], d_scales[:], vt_d[:])
+        gather(True, listed_a, pool_a, 0, A_SHARE)
         row_factor = sbuf("row_factor", [P, PACK], F32)
         nc.vector.tensor_tensor(out=row_factor[:], in0=inv_sum[:], in1=fac_sb[:], op=ALU.mult)
-        gather(True, listed_a, pool_a, 0, A_SHARE)
+        d_codes, d_scales = mx_tiles("d", NARROW, 4 * WINDOW)
+        quantize(d_codes[:], d_scales[:], vt_d[:])
         gather(False, listed_a, pool_a, A_SHARE, I)
         nc.sync.dma_start(out=pool_a[NARROW_ROWS, :], in_=vals[E - NARROW : E, :])
 

@@ -133,8 +133,7 @@ def tile_attend_slotattn_kernel(tc, query, keys_words, keys_scales, fac, vals, o
         words_a = listed_a[:].bitcast(F32)
         vt_d = sbuf("vt_d", [P, NARROW, PACK], BF16)
         words_d = vt_d[:].rearrange("p e t -> p (e t)").bitcast(F32)
-        last_max = sbuf("last_max", [P, 1], F32)
-        neg_max = [words_a[:, 0:1], words_a[:, I // 4 - 1 : I // 4], words_d[:, 0:1], last_max[:]]
+        neg_max = [words_a[:, 0:1], words_a[:, 1:2], words_d[:, 0:1], words_a[:, I // 4 : I // 4 + 1]]
         row_sum = sbuf("row_sum", [P, PACK], F32, 4 * WINDOW)
         probs = sbuf("probs", [P, PACK, Q], F32, 0)
         for t in range(PACK):

@@ -43,10 +43,10 @@ def tile_attend_slotattn_kernel(tc, query, keys_words, keys_scales, fac, vals, o
         turns = ctx.enter_context(tc.tile_pool(name="turns", bufs=1))
         psum = ctx.enter_context(tc.psum_pool(name="psum", bufs=1))
 
-        def sbuf(name, shape, dtype, at=None):
+        def sbuf(name, shape, dtype, at=None, align=64):
             if at is None:
-                return keep.tile(shape, dtype, name=name, align_bytes=64)
-            return turns.tile(shape, dtype, name=name, align_bytes=64, offset=at)
+                return keep.tile(shape, dtype, name=name, align_bytes=align)
+            return turns.tile(shape, dtype, name=name, align_bytes=256, offset=at)
 
         def bank(name, shape, number):
             return psum.tile(shape, F32, name=name, tag=f"bank{number}")
@@ -56,7 +56,7 @@ def tile_attend_slotattn_kernel(tc, query, keys_words, keys_scales, fac, vals, o
         fac_sb = sbuf("fac_sb", [P, PACK], F32)
         nc.sync.dma_start(out=fac_sb[:], in_=fac.rearrange("(p t) o -> p (t o)", t=PACK))
 
-        q_raw = sbuf("q_raw", [P, PACK, Q], F32)
+        q_raw = sbuf("q_raw", [P, PACK, Q], F32, align=256)
         nc.scalar.dma_start(out=q_raw[:], in_=query.rearrange("(p j) q -> p j q", j=PACK))
 
         ks_pool = sbuf("ks_pool", [P, T], U8, 2 * WINDOW)
@@ -238,13 +238,13 @@ def tile_attend_slotattn_kernel(tc, query, keys_words, keys_scales, fac, vals, o
             product(c_acc[h][:], h, c_codes[:], c_scales[:])
         e_codes, e_scales = mx_tiles("e", NARROW)
         quantize(e_codes[:], e_scales[:], vt_e[:])
-        c_out = sbuf("c_out", [P, HALVES, P], F32)
+        c_out = sbuf("c_out", [P, HALVES, P], F32, align=256)
         for h in range(HALVES):
             paths[h][0](out=c_out[:, h, :], in_=c_acc[h][:])
         nc.sync.dma_start(out=out_rows[:, :, early : early + P], in_=c_out[:])
         for h, (copy, queue) in enumerate(paths):
             e_acc = bank(f"e_acc{h}", [P, NARROW], 6 + h)
             product(e_acc[:], h, e_codes[:], e_scales[:])
-            e_out = sbuf(f"e_out{h}", [P, NARROW], F32)
+            e_out = sbuf(f"e_out{h}", [P, NARROW], F32, align=256)
             copy(out=e_out[:], in_=e_acc[:])
             queue.dma_start(out=out_rows[:, h, E - NARROW : E], in_=e_out[:])

from contextlib import ExitStack

import concourse.mybir as mybir
from concourse.masks import make_identity

D, T, I, Q, E = 512, 2048, 512, 256, 512
FLOPS = 2 * D * I * Q + 2 * I * Q * E

F32 = mybir.dt.float32
BF16 = mybir.dt.bfloat16
I32 = mybir.dt.int32
U32 = mybir.dt.uint32
U16 = mybir.dt.uint16
U8 = mybir.dt.uint8
FP8X4 = mybir.dt.float8_e4m3fn_x4
ALU = mybir.AluOpType
ACT = mybir.ActivationFunctionType
AX = mybir.AxisListType

P = 128
PACK = 4
HALVES = Q // P
WINDOW = 4 * T
NARROW = 64
NARROW_ROWS = slice(32, 96)
EVEN_SHARE = I // 2
A_SHARE = 64
B_SHARE = 224
C_SHARE = 192


def interleave(copy, dst, src):
    copy(
        out=dst.rearrange("p (c i) t -> p c t i", i=4),
        in_=src.rearrange("p t (c i) -> p c t i", i=4),
    )


def tile_attend_slotattn_kernel(tc, query, keys_words, keys_scales, fac, vals, offs, out):
    nc = tc.nc
    with ExitStack() as ctx:
        keep = ctx.enter_context(tc.tile_pool(name="keep", bufs=1))
        turns = ctx.enter_context(tc.tile_pool(name="turns", bufs=1))
        psum = ctx.enter_context(tc.psum_pool(name="psum", bufs=1))

        def sbuf(name, shape, dtype, at=None, align=64):
            if at is None:
                return keep.tile(shape, dtype, name=name, align_bytes=align)
            return turns.tile(shape, dtype, name=name, align_bytes=256, offset=at)

        def bank(name, shape, number):
            return psum.tile(shape, F32, name=name, tag=f"bank{number}")

        offsets = keep.tile([P, I // 16], U16, name="offsets")
        nc.sync.dma_start(offsets[:], offs)
        fac_sb = sbuf("fac_sb", [P, PACK], F32)
        nc.sync.dma_start(out=fac_sb[:], in_=fac.rearrange("(p t) o -> p (t o)", t=PACK))

        q_raw = sbuf("q_raw", [P, PACK, Q], F32, align=256)
        nc.scalar.dma_start(out=q_raw[:], in_=query.rearrange("(p j) q -> p j q", j=PACK))

        ks_pool = sbuf("ks_pool", [P, T], U8, 2 * WINDOW)
        nc.vector.memset(ks_pool[:].bitcast(I32), 0)
        for r in range(4):
            nc.sync.dma_start(
                out=ks_pool[r:P:32, :].bitcast(I32),
                in_=keys_scales[0, r:16:4, :].bitcast(I32),
            )

        kw_pool = sbuf("kw_pool", [P, T], U32, 3 * WINDOW)
        nc.sync.dma_start(
            out=kw_pool[:].bitcast(I32),
            in_=keys_words[0].rearrange("p n t -> p (n t)").bitcast(I32),
        )

        k_scales = sbuf("k_scales", [P, PACK, P], U8)
        ident = sbuf("ident", [P, P], F32)
        nc.vector.memset(ident[:], 0.0)
        make_identity(nc, ident[:], nomemset=True)

        narrow_pool = sbuf("narrow_pool", [P, T], F32, 0)
        nc.vector.memset(narrow_pool[:], 0.0)
        nc.sync.dma_start(out=narrow_pool[NARROW_ROWS, :], in_=vals[0:NARROW, :])

        def load_wide(c):
            pool = sbuf(f"wide_pool{c}", [P, T], F32, (c + 1) * WINDOW)
            nc.sync.dma_start(out=pool[:], in_=vals[NARROW + c * P : NARROW + (c + 1) * P, :])
            return pool

        def gather(on_vector, listed, pool, lo, hi):
            window = pool[:].indirect(offsets[:, lo // 16 : hi // 16])
            if on_vector:
                nc.vector.tensor_copy(listed[:, lo:hi], window)
            else:
                nc.scalar.activation(listed[:, lo:hi], window, ACT.Copy)

        def gather_shared(name, pool, share):
            listed = sbuf(name, [P, I], BF16)
            gather(True, listed, pool, 0, share)
            gather(False, listed, pool, share, I)
            return listed

        def transposed(name, listed, number):
            pairs = listed[:].bitcast(F32)
            turned = bank(name, [P, 2, P], number)
            for u in range(2):
                nc.tensor.transpose(turned[:, u, :], pairs[:, u : I // 2 : 2], ident[:])
            return turned

        def weave(copy, vt_bf, turned):
            copy(out=vt_bf.bitcast(F32), in_=turned.rearrange("p u e -> p e u"))

        def quantize(codes, scales, values):
            nc.vector.quantize_mx(out=codes.bitcast(FP8X4), scales=scales, in_=values.rearrange("p e t -> p (e t)"))

        def mx_tiles(name, width, at=None):
            return sbuf(name + "_codes", [P, width], U32, at), sbuf(name + "_scales", [P, width], U8)

        q_bf = sbuf("q_bf", [P, Q, PACK], BF16)
        interleave(nc.scalar.copy, q_bf[:], q_raw[:])
        nc.vector.tensor_copy(k_scales[:].rearrange("p t s -> p s t"), ks_pool[:].indirect(offsets[:]))
        q_codes, q_scales = mx_tiles("q", Q)
        quantize(q_codes[:], q_scales[:], q_bf[:])
        pool_a = load_wide(0)
        pool_b = load_wide(1)
        k_codes = sbuf("k_codes", [P, PACK, P], U32)
        nc.vector.tensor_copy(k_codes[:].rearrange("p t s -> p s t"), kw_pool[:].indirect(offsets[:]))
        pool_c = load_wide(2)
        listed_d = sbuf("listed_d", [P, I], BF16)
        gather(False, listed_d, narrow_pool, 0, I)

        listed_a = sbuf("listed_a", [P, I], BF16)
        words_a = listed_a[:].bitcast(F32)
        vt_d = sbuf("vt_d", [P, NARROW, PACK], BF16)
        words_d = vt_d[:].rearrange("p e t -> p (e t)").bitcast(F32)
        neg_max = [words_a[:, 0:1], words_a[:, 1:2], words_d[:, 0:1], words_a[:, I // 4 : I // 4 + 1]]
        row_sum = sbuf("row_sum", [P, PACK], F32, 4 * WINDOW)
        probs = sbuf("probs", [P, PACK, Q], F32, 0)
        for t in range(PACK):
            scores = bank(f"scores{t}", [P, Q], t)
            nc.tensor.matmul_mx(
                out=scores[:],
                lhsT=k_codes[:, t, :].bitcast(FP8X4),
                lhsT_scale=k_scales[:, t, :],
                rhs=q_codes[:].bitcast(FP8X4),
                rhs_scale=q_scales[:],
                start=True,
                stop=True,
            )
            nc.vector.tensor_reduce(out=neg_max[t], in_=scores[:], axis=AX.X, op=ALU.max, negate=True)
            nc.scalar.activation(
                out=probs[:, t, :],
                in_=scores[:],
                func=ACT.Exp,
                bias=neg_max[t],
                accum_out=row_sum[:, t : t + 1],
            )

        turned_d = transposed("turned_d", listed_d, 4)
        weave(nc.vector.tensor_copy, vt_d[:], turned_d[:, :, NARROW_ROWS])
        inv_sum = sbuf("inv_sum", [P, PACK], F32)
        nc.vector.reciprocal(out=inv_sum[:], in_=row_sum[:])
        gather(True, listed_a, pool_a, 0, A_SHARE)
        row_factor = sbuf("row_factor", [P, PACK], F32)
        nc.vector.tensor_tensor(out=row_factor[:], in0=inv_sum[:], in1=fac_sb[:], op=ALU.mult)
        d_codes, d_scales = mx_tiles("d", NARROW, 4 * WINDOW)
        quantize(d_codes[:], d_scales[:], vt_d[:])
        gather(False, listed_a, pool_a, A_SHARE, I)
        nc.sync.dma_start(out=pool_a[NARROW_ROWS, :], in_=vals[E - NARROW : E, :])

        def weights(h, at):
            w_bf = sbuf(f"w_bf{h}", [P, P, PACK], BF16, at)
            nc.vector.tensor_tensor(
                out=w_bf[:].rearrange("p (c i) t -> p c t i", i=4),
                in0=probs[:, :, h * P : (h + 1) * P].rearrange("p t (c i) -> p c t i", i=4),
                in1=row_factor[:].unsqueeze(1).unsqueeze(3).to_broadcast([P, P // 4, PACK, 4]),
                op=ALU.mult,
            )
            return w_bf

        w_low = weights(0, None)
        turned_a = transposed("turned_a", listed_a, 5)
        listed_b = gather_shared("listed_b", pool_b, B_SHARE)
        w_high = weights(1, 2 * WINDOW + 2048)
        vt_a = sbuf("vt_a", [P, P, PACK], BF16, 2 * WINDOW + 1024)
        weave(nc.scalar.copy, vt_a[:], turned_a[:])
        w_codes, w_scales = mx_tiles("w", Q, 2 * WINDOW)
        for h, w_bf in enumerate((w_low, w_high)):
            quantize(w_codes[:, h * P : (h + 1) * P], w_scales[:, h * P : (h + 1) * P], w_bf[:])
        ab_codes, ab_scales = mx_tiles("ab", 2 * P)
        quantize(ab_codes[:, 0:P], ab_scales[:, 0:P], vt_a[:])
        vt_b = sbuf("vt_b", [P, P, PACK], BF16)
        weave(nc.scalar.copy, vt_b[:], transposed("turned_b", listed_b, 0)[:])
        quantize(ab_codes[:, P : 2 * P], ab_scales[:, P : 2 * P], vt_b[:])

        out_rows = out.rearrange("(h p) e -> p h e", p=P)

        def product(acc, h, v_codes, v_scales):
            nc.tensor.matmul_mx(
                out=acc,
                lhsT=w_codes[:, h * P : (h + 1) * P].bitcast(FP8X4),
                lhsT_scale=w_scales[:, h * P : (h + 1) * P],
                rhs=v_codes.bitcast(FP8X4),
                rhs_scale=v_scales,
                start=True,
                stop=True,
            )

        paths = ((nc.vector.tensor_copy, nc.sync), (nc.scalar.copy, nc.scalar))
        early = NARROW + 2 * P
        early_acc = [bank(f"early_acc{h}", [P, early], 2 + h) for h in range(HALVES)]
        for h in range(HALVES):
            product(early_acc[h][:, 0:NARROW], h, d_codes[:], d_scales[:])
        for c in range(2):
            for h in range(HALVES):
                cols = slice(c * P, (c + 1) * P)
                product(early_acc[h][:, NARROW + c * P : NARROW + (c + 1) * P], h, ab_codes[:, cols], ab_scales[:, cols])
        listed_c = gather_shared("listed_c", pool_c, C_SHARE)
        turned_c = transposed("turned_c", listed_c, 1)

        def store_early(h):
            early_out = sbuf(f"early_out{h}", [P, early], F32, 1 * WINDOW + (2 - h) * 2048)
            paths[h][0](out=early_out[:], in_=early_acc[h][:])
            nc.sync.dma_start(out=out_rows[:, h, 0:early], in_=early_out[:])

        listed_e = gather_shared("listed_e", pool_a, EVEN_SHARE)
        turned_e = transposed("turned_e", listed_e, 4)
        vt_c = sbuf("vt_c", [P, P, PACK], BF16, 1 * WINDOW)
        weave(nc.scalar.copy, vt_c[:], turned_c[:])
        c_codes, c_scales = mx_tiles("c", P)
        store_early(0)
        quantize(c_codes[:], c_scales[:], vt_c[:])
        store_early(1)
        vt_e = sbuf("vt_e", [P, NARROW, PACK], BF16)
        weave(nc.scalar.copy, vt_e[:], turned_e[:, :, NARROW_ROWS])
        c_acc = [bank(f"c_acc{h}", [P, P], 5 * h) for h in range(HALVES)]
        for h in range(HALVES):
            product(c_acc[h][:], h, c_codes[:], c_scales[:])
        e_codes, e_scales = mx_tiles("e", NARROW)
        quantize(e_codes[:], e_scales[:], vt_e[:])
        c_out = sbuf("c_out", [P, HALVES, P], F32, align=256)
        for h in range(HALVES):
            paths[h][0](out=c_out[:, h, :], in_=c_acc[h][:])
        nc.sync.dma_start(out=out_rows[:, :, early : early + P], in_=c_out[:])
        for h, (copy, queue) in enumerate(paths):
            e_acc = bank(f"e_acc{h}", [P, NARROW], 6 + h)
            product(e_acc[:], h, e_codes[:], e_scales[:])
            e_out = sbuf(f"e_out{h}", [P, NARROW], F32, align=256)
            copy(out=e_out[:], in_=e_acc[:])
            queue.dma_start(out=out_rows[:, h, E - NARROW : E], in_=e_out[:])
